import numpy as np
import ml_dtypes


def mxq(x, axis, fmt="e4m3"):
    dtype, down = {"e4m3": (ml_dtypes.float8_e4m3fn, 7), "e5m2": (ml_dtypes.float8_e5m2, 14)}[fmt]
    v = np.moveaxis(np.asarray(x, np.float32).astype(ml_dtypes.bfloat16).astype(np.float64), axis, -1)
    blocks = v.reshape(v.shape[:-1] + (-1, 32))
    amax = np.abs(blocks).max(-1, keepdims=True)
    byte = np.maximum(np.where(amax > 0, np.frexp(amax)[1] - 1 + 127, 0) - down, 1)
    scale = np.exp2(byte - 127.0)
    codes = (blocks / scale).astype(np.float32).astype(dtype).astype(np.float64)
    return np.moveaxis((codes * scale).reshape(v.shape), -1, axis)


WIDE = False


def mx_kscale(k):
    if not WIDE:
        return np.ones(k)
    levels = np.array([10, -10, 5, -5, 0])
    if k % 512:
        return np.exp2(np.random.permutation(np.resize(levels, k // 32))).repeat(32)
    a = np.empty((k // 512, 16))
    for p in range(k // 512):
        a[p, :8] = np.random.permutation(np.resize(levels, 8))
        for g in range(8):
            far = levels[np.abs(levels - a[p, g]) >= 10]
            a[p, g + 8] = far[np.random.randint(len(far))]
    return np.exp2(a.ravel()).repeat(32)


def f64(x):
    return np.asarray(x).astype(np.float64)


def striped(idx):
    return np.tile(np.asarray(idx).reshape(-1, 16).T, (8, 1)).astype(np.uint16)


def unstriped(offs):
    return offs[:16].T.reshape(-1).astype(np.int64)


B, N, T, D, DV, NQ = 1, 512, 2048, 512, 512, 256
CAP = 2.0


def setup_inputs():
    n = np.random.standard_normal
    idx = np.sort(np.random.permutation(T)[:B * N].reshape(B, N), axis=1).reshape(-1)
    s = mx_kscale(D)[:, None]
    u = np.ones(T)
    u[idx] = mx_kscale(B * N)
    r = np.random.uniform(0.5, 2.0, T)
    raw = n((D, T)) / s / (u * r)
    return {
        "qT": (n((B, D, NQ)) * s * (0.80 / np.sqrt(D))).astype(np.float32),
        "cT": raw.astype(np.float32),
        "ts": np.tile(u * r, (128, 1)).astype(np.float32),
        "ch": np.tile(s[:, 0] * np.random.uniform(0.5, 2.0, D), (128, 1)).astype(np.float32),
        "offs": striped(idx),
    }


def reference(qT, cT, ts, ch, offs):
    idx = unstriped(offs)
    c = f64(cT)
    pick = lambda x: x[:, idx].reshape(x.shape[0], B, N).transpose(1, 0, 2)
    q = f64(qT)
    score = mxq(q, 1, "e4m3").transpose(0, 2, 1) @ mxq(pick(c), 1, "e4m3")
    score = score * pick(f64(ts))[:, :1, :]
    score = CAP * np.tanh(score / CAP)
    m = score.max(-1, keepdims=True)
    p = np.exp(score - m)
    total = p.sum(-1, keepdims=True)
    w = p * pick(f64(ts))[:, :1, :]
    y = mxq(w, 2, "e4m3") @ mxq(pick(c).transpose(0, 2, 1), 1, "e4m3")
    y = y / total
    y = y * f64(ch)[:1]
    return y

@@ -1,0 +1,216 @@
+from contextlib import ExitStack
+
+import concourse.mybir as mybir
+from concourse.masks import make_identity
+
+F32 = mybir.dt.float32
+BF16 = mybir.dt.bfloat16
+U32 = mybir.dt.uint32
+U16 = mybir.dt.uint16
+U8 = mybir.dt.uint8
+FP8X4 = mybir.dt.float8_e4m3fn_x4
+ACT = mybir.ActivationFunctionType
+ALU = mybir.AluOpType
+AX = mybir.AxisListType
+
+P = 128
+PACK = 4
+TOKENS = 2048
+SLOTS = 512
+QUERIES = 256
+FEATURES = 512
+BLOCKS = QUERIES // P
+HALF = SLOTS // 2
+CAP = 2.0
+
+FLOPS = 2 * 2 * QUERIES * SLOTS * FEATURES
+
+
+def tile_attend_x_mla_cap_srt_kernel(tc, qT, cT, ts, ch, offs, out):
+    nc = tc.nc
+    with ExitStack() as ctx:
+        keep = ctx.enter_context(tc.tile_pool(name="keep", bufs=1))
+        psum_t = ctx.enter_context(tc.psum_pool(name="psum_t", bufs=2))
+        psum = ctx.enter_context(tc.psum_pool(name="psum", bufs=1))
+
+        offsets = keep.tile([P, SLOTS // 16], U16, name="offsets")
+        nc.sync.dma_start(offsets[:], offs)
+
+        plane_rows = cT.rearrange("(p j) w -> j p w", j=PACK)
+        early = keep.tile([P, 2, TOKENS], F32, name="early")
+        late = keep.tile([P, 2, TOKENS], F32, name="late")
+        planes = [early[:, 0, :], early[:, 1, :], late[:, 0, :], late[:, 1, :]]
+        for t in range(2):
+            nc.sync.dma_start(planes[t], plane_rows[t])
+        ts_row = keep.tile([P, TOKENS], F32, name="ts_row")
+        nc.vector.memset(ts_row[:], 0.0)
+        nc.scalar.dma_start(ts_row[0:1, :], ts[0:1, :])
+        q_raw = keep.tile([P, PACK, QUERIES], F32, name="q_raw")
+        channel = keep.tile([P, FEATURES], F32, name="channel")
+        nc.vector.memset(late[:, :, 0:1], 0.0)
+        nc.vector.memset(q_raw[:, :, 0:1], 0.0)
+        nc.vector.memset(channel[:, 0:1], 0.0)
+        for t in range(2, PACK):
+            nc.sync.dma_start(planes[t], plane_rows[t])
+        nc.sync.dma_start(q_raw[:], qT[0].rearrange("(p j) q -> p j q", j=PACK))
+        nc.sync.dma_start(channel[:], ch)
+
+        ident32 = keep.tile([P, P], F32, name="ident32")
+        make_identity(nc, ident32[:])
+        ident16 = keep.tile([P, P], BF16, name="ident16")
+        make_identity(nc, ident16[:])
+        warm = keep.tile([P, 1], F32, name="warm")
+        nc.vector.memset(warm[:], 0.0)
+        nc.scalar.activation(warm[:], warm[:], ACT.Exp)
+
+        k_quads = keep.tile([P, SLOTS, PACK], BF16, name="k_quads", align_bytes=64)
+        k_codes = keep.tile([P, SLOTS], U32, name="k_codes", align_bytes=64)
+        k_scales = keep.tile([P, SLOTS], U8, name="k_scales", align_bytes=64)
+        v_quads = keep.tile([P, FEATURES, PACK], BF16, name="v_quads", align_bytes=64)
+        v_codes = keep.tile([P, FEATURES], U32, name="v_codes", align_bytes=64)
+        v_scales = keep.tile([P, FEATURES], U8, name="v_scales", align_bytes=64)
+        q_quads = keep.tile([P, QUERIES, PACK], BF16, name="q_quads", align_bytes=64)
+        q_codes = keep.tile([P, QUERIES], U32, name="q_codes", align_bytes=64)
+        q_scales = keep.tile([P, QUERIES], U8, name="q_scales", align_bytes=64)
+        w_quads = keep.tile([P, QUERIES, PACK], BF16, name="w_quads", align_bytes=64)
+        w_codes = keep.tile([P, QUERIES], U32, name="w_codes", align_bytes=64)
+        w_scales = keep.tile([P, QUERIES], U8, name="w_scales", align_bytes=64)
+
+        def quantize(codes, scales, quads, lo, hi):
+            nc.vector.quantize_mx(
+                out=codes[:, lo:hi].bitcast(FP8X4),
+                scales=scales[:, lo:hi],
+                in_=quads[:, lo:hi, :].rearrange("p n j -> p (n j)"),
+            )
+
+        by_place = k_quads[:].rearrange("p (s i) t -> p t i s", i=PACK)
+
+        def turn_plane(t, copy, turned):
+            for i in range(PACK):
+                nc.tensor.transpose(turned[:, i, :], by_place[:, t, i, :], ident16[:])
+            copy(v_quads[:, t * P : (t + 1) * P, :], turned[:].rearrange("s i p -> s p i"))
+
+        def gather_plane(t):
+            nc.vector.tensor_copy(k_quads[:, :, t], planes[t].indirect(offsets[:]))
+
+        gather_plane(0)
+        turn_plane(0, nc.scalar.copy, psum_t.tile([P, PACK, P], BF16, name="turned"))
+        gather_plane(1)
+        turn_plane(1, nc.scalar.copy, psum_t.tile([P, PACK, P], BF16, name="turned"))
+        ts_slots = keep.tile([P, SLOTS], F32, name="ts_slots")
+        nc.vector.tensor_copy(ts_slots[:], ts_row[:].indirect(offsets[:]))
+        ts_turned = psum_t.tile([P, PACK, P], F32, name="ts_turned", tag="turned")
+        for i in range(PACK):
+            nc.tensor.transpose(ts_turned[:, i, :], ts_slots[:, i:SLOTS:PACK], ident32[:])
+        ts_column = keep.tile([P, PACK], F32, name="ts_column")
+        nc.scalar.copy(ts_column[:], ts_turned[:, :, 0])
+        ts_spread = psum_t.tile([P, SLOTS], F32, name="ts_spread", tag="turned")
+        for i in range(PACK):
+            nc.tensor.transpose(ts_spread[:, i * P : (i + 1) * P], ts_column[:, i : i + 1].to_broadcast([P, P]), ident32[:])
+        ts_all = keep.tile([P, SLOTS], F32, name="ts_all")
+        nc.scalar.copy(ts_all[:], ts_spread[:])
+
+        gather_plane(2)
+
+        def gather_last(h):
+            nc.vector.tensor_copy(
+                k_quads[:, h * HALF : (h + 1) * HALF, 3],
+                planes[3].indirect(offsets[:, h * HALF // 16 : (h + 1) * HALF // 16]),
+            )
+
+        gather_last(0)
+        gather_last(1)
+        for b in range(BLOCKS):
+            rows = slice(b * P, (b + 1) * P)
+            nc.scalar.copy(q_quads[:, rows, :], q_raw[:, :, rows].rearrange("p j q -> p q j"))
+        scores, total, prob = [], [], []
+        for b in range(BLOCKS):
+            scores.append(psum.tile([P, SLOTS], F32, name=f"scores{b}"))
+            total.append(keep.tile([P, 1], F32, name=f"total{b}"))
+            prob.append(keep.tile([P, PACK, P], F32, name=f"prob{b}"))
+        for h in range(2):
+            quantize(k_codes, k_scales, k_quads, h * HALF, (h + 1) * HALF)
+        for b in range(BLOCKS):
+            rows = slice(b * P, (b + 1) * P)
+            quantize(q_codes, q_scales, q_quads, b * P, (b + 1) * P)
+            if b == 0:
+                quantize(v_codes, v_scales, v_quads, 0, 2 * P)
+            nc.tensor.matmul_mx(
+                out=scores[b][:],
+                lhsT=q_codes[:, rows].bitcast(FP8X4),
+                lhsT_scale=q_scales[:, rows],
+                rhs=k_codes[:].bitcast(FP8X4),
+                rhs_scale=k_scales[:],
+                start=True,
+                stop=True,
+            )
+        scaled, capped, minus_m = [], [], []
+        for b in range(BLOCKS):
+            scaled.append(keep.tile([P, PACK, P], F32, name=f"scaled{b}"))
+            capped.append(keep.tile([P, PACK, P], F32, name=f"capped{b}"))
+            minus_m.append(keep.tile([P, 1], F32, name=f"minus_m{b}"))
+        for b in range(BLOCKS):
+            nc.vector.tensor_tensor(
+                scaled[b][:],
+                scores[b][:].rearrange("q (s i) -> q i s", i=PACK),
+                ts_all[:].rearrange("q (i s) -> q i s", i=PACK),
+                ALU.mult,
+            )
+            nc.scalar.activation(capped[b][:], scaled[b][:], ACT.Tanh, scale=1.0 / CAP)
+        for b in range(BLOCKS):
+            top = keep.tile([P, 1], F32, name=f"top{b}")
+            nc.vector.tensor_reduce(top[:], scaled[b][:].rearrange("q i s -> q (i s)"), AX.X, ALU.max)
+            pair = keep.tile([P, 2], F32, name=f"pair{b}")
+            nc.scalar.activation(
+                pair[:], top[:].to_broadcast([P, 2]), ACT.Tanh, scale=-1.0 / CAP, accum_out=minus_m[b][:]
+            )
+            nc.scalar.activation(
+                prob[b][:], capped[b][:], ACT.Exp, bias=minus_m[b][:], scale=CAP, accum_out=total[b][:]
+            )
+        for t in range(2, PACK):
+            turn_plane(t, nc.vector.tensor_copy, psum.tile([P, PACK, P], BF16, name=f"turned{t}", tag=f"scores{t - 2}"))
+        turned_prob = []
+        for b in range(BLOCKS):
+            turned_prob.append(psum.tile([P, PACK, P], F32, name=f"turned_prob{b}"))
+            for i in range(PACK):
+                nc.tensor.transpose(turned_prob[b][:, i, :], prob[b][:, i, :], ident32[:])
+        quantize(v_codes, v_scales, v_quads, 2 * P, 3 * P)
+        for b in range(BLOCKS):
+            nc.vector.tensor_tensor(
+                w_quads[:, b * P : (b + 1) * P, :],
+                turned_prob[b][:].rearrange("s i q -> s q i"),
+                ts_column[:].unsqueeze(1).to_broadcast([P, P, PACK]),
+                ALU.mult,
+            )
+        quantize(v_codes, v_scales, v_quads, 3 * P, 4 * P)
+        y = []
+        for b in range(BLOCKS):
+            rows = slice(b * P, (b + 1) * P)
+            quantize(w_codes, w_scales, w_quads, b * P, (b + 1) * P)
+            y.append(psum.tile([P, FEATURES], F32, name=f"y{b}"))
+            nc.tensor.matmul_mx(
+                out=y[b][:],
+                lhsT=w_codes[:, rows].bitcast(FP8X4),
+                lhsT_scale=w_scales[:, rows],
+                rhs=v_codes[:].bitcast(FP8X4),
+                rhs_scale=v_scales[:],
+                start=True,
+                stop=True,
+            )
+        for b in range(BLOCKS):
+            rows = slice(b * P, (b + 1) * P)
+            inverse = keep.tile([P, 1], F32, name=f"inverse{b}")
+            nc.vector.reciprocal(inverse[:], total[b][:])
+            result = keep.tile([P, P, PACK], F32, name=f"result{b}")
+            pieces = 1 if b == 0 else 2
+            for piece in range(pieces):
+                part = slice(piece * P // pieces, (piece + 1) * P // pieces)
+                nc.vector.scalar_tensor_tensor(
+                    result[:, part, :],
+                    y[b][:].rearrange("q (t p) -> q p t", t=PACK)[:, part, :],
+                    inverse[:],
+                    channel[:].rearrange("q (p t) -> q p t", t=PACK)[:, part, :],
+                    ALU.mult,
+                    ALU.mult,
+                )
+                nc.sync.dma_start(out[0, rows, :].rearrange("q (p t) -> q p t", t=PACK)[:, part, :], result[:, part, :])

@@ -21,6 +21,8 @@ QUERIES = 256
 FEATURES = 512
 BLOCKS = QUERIES // P
 HALF = SLOTS // 2
+BANK = 512
+PREFIX = TOKENS - HALF
 CAP = 2.0
 
 FLOPS = 2 * 2 * QUERIES * SLOTS * FEATURES
@@ -30,187 +32,208 @@ def tile_attend_x_mla_cap_srt_kernel(tc, qT, cT, ts, ch, offs, out):
     nc = tc.nc
     with ExitStack() as ctx:
         keep = ctx.enter_context(tc.tile_pool(name="keep", bufs=1))
-        psum_t = ctx.enter_context(tc.psum_pool(name="psum_t", bufs=2))
+        shared = ctx.enter_context(tc.tile_pool(name="shared", bufs=1))
         psum = ctx.enter_context(tc.psum_pool(name="psum", bufs=1))
 
+        per_row = TOKENS // P
+        ts_rows = keep.tile([P, per_row], F32, name="ts_rows")
+        nc.sync.dma_start(ts_rows[:], ts[0].rearrange("(p c) -> p c", c=per_row))
+        plane_rows = cT.rearrange("(p j) w -> j p w", j=PACK)
+        planes = [keep.tile([P, TOKENS], F32, name=f"plane{t}", align_bytes=64) for t in range(PACK)]
+        nc.sync.dma_start(planes[2][:], plane_rows[2])
         offsets = keep.tile([P, SLOTS // 16], U16, name="offsets")
         nc.sync.dma_start(offsets[:], offs)
-
-        plane_rows = cT.rearrange("(p j) w -> j p w", j=PACK)
-        early = keep.tile([P, 2, TOKENS], F32, name="early")
-        late = keep.tile([P, 2, TOKENS], F32, name="late")
-        planes = [early[:, 0, :], early[:, 1, :], late[:, 0, :], late[:, 1, :]]
         for t in range(2):
-            nc.sync.dma_start(planes[t], plane_rows[t])
-        ts_row = keep.tile([P, TOKENS], F32, name="ts_row")
-        nc.vector.memset(ts_row[:], 0.0)
-        nc.scalar.dma_start(ts_row[0:1, :], ts[0:1, :])
-        q_raw = keep.tile([P, PACK, QUERIES], F32, name="q_raw")
+            nc.sync.dma_start(planes[t][:], plane_rows[t])
+        nc.sync.dma_start(planes[3][:, :PREFIX], plane_rows[3][:, :PREFIX])
+        nc.sync.dma_start(planes[3][:, PREFIX:], plane_rows[3][:, PREFIX:])
+        q_rows = qT[0].rearrange("(p j) q -> p j q", j=PACK)
+        q_raw = []
+        for b in range(BLOCKS):
+            q_raw.append(keep.tile([P, PACK, P], F32, name=f"q_raw{b}", align_bytes=64))
+            nc.sync.dma_start(q_raw[b][:], q_rows[:, :, b * P : (b + 1) * P])
         channel = keep.tile([P, FEATURES], F32, name="channel")
-        nc.vector.memset(late[:, :, 0:1], 0.0)
-        nc.vector.memset(q_raw[:, :, 0:1], 0.0)
-        nc.vector.memset(channel[:, 0:1], 0.0)
-        for t in range(2, PACK):
-            nc.sync.dma_start(planes[t], plane_rows[t])
-        nc.sync.dma_start(q_raw[:], qT[0].rearrange("(p j) q -> p j q", j=PACK))
         nc.sync.dma_start(channel[:], ch)
 
-        ident32 = keep.tile([P, P], F32, name="ident32")
-        make_identity(nc, ident32[:])
-        ident16 = keep.tile([P, P], BF16, name="ident16")
-        make_identity(nc, ident16[:])
+        ident = keep.tile([P, P], F32, name="ident")
+        make_identity(nc, ident[:])
         warm = keep.tile([P, 1], F32, name="warm")
         nc.vector.memset(warm[:], 0.0)
         nc.scalar.activation(warm[:], warm[:], ACT.Exp)
 
-        k_quads = keep.tile([P, SLOTS, PACK], BF16, name="k_quads", align_bytes=64)
-        k_codes = keep.tile([P, SLOTS], U32, name="k_codes", align_bytes=64)
-        k_scales = keep.tile([P, SLOTS], U8, name="k_scales", align_bytes=64)
-        v_quads = keep.tile([P, FEATURES, PACK], BF16, name="v_quads", align_bytes=64)
-        v_codes = keep.tile([P, FEATURES], U32, name="v_codes", align_bytes=64)
-        v_scales = keep.tile([P, FEATURES], U8, name="v_scales", align_bytes=64)
-        q_quads = keep.tile([P, QUERIES, PACK], BF16, name="q_quads", align_bytes=64)
-        q_codes = keep.tile([P, QUERIES], U32, name="q_codes", align_bytes=64)
-        q_scales = keep.tile([P, QUERIES], U8, name="q_scales", align_bytes=64)
-        w_quads = keep.tile([P, QUERIES, PACK], BF16, name="w_quads", align_bytes=64)
-        w_codes = keep.tile([P, QUERIES], U32, name="w_codes", align_bytes=64)
-        w_scales = keep.tile([P, QUERIES], U8, name="w_scales", align_bytes=64)
+        def operand(name, width, tag=None):
+            codes = keep.tile([P, width], U32, name=f"{name}_codes", tag=tag or f"{name}_codes", align_bytes=64)
+            scales = keep.tile([P, width], U8, name=f"{name}_scales", align_bytes=64)
+            return codes, scales
 
-        def quantize(codes, scales, quads, lo, hi):
+        def quantize(target, quads, lo=0):
+            hi = lo + quads.shape[1]
             nc.vector.quantize_mx(
-                out=codes[:, lo:hi].bitcast(FP8X4),
-                scales=scales[:, lo:hi],
-                in_=quads[:, lo:hi, :].rearrange("p n j -> p (n j)"),
+                out=target[0][:, lo:hi].bitcast(FP8X4),
+                scales=target[1][:, lo:hi],
+                in_=quads.rearrange("p n j -> p (n j)"),
             )
 
-        by_place = k_quads[:].rearrange("p (s i) t -> p t i s", i=PACK)
-
-        def turn_plane(t, copy, turned):
-            for i in range(PACK):
-                nc.tensor.transpose(turned[:, i, :], by_place[:, t, i, :], ident16[:])
-            copy(v_quads[:, t * P : (t + 1) * P, :], turned[:].rearrange("s i p -> s p i"))
-
-        def gather_plane(t):
-            nc.vector.tensor_copy(k_quads[:, :, t], planes[t].indirect(offsets[:]))
-
-        gather_plane(0)
-        turn_plane(0, nc.scalar.copy, psum_t.tile([P, PACK, P], BF16, name="turned"))
-        gather_plane(1)
-        turn_plane(1, nc.scalar.copy, psum_t.tile([P, PACK, P], BF16, name="turned"))
-        ts_slots = keep.tile([P, SLOTS], F32, name="ts_slots")
-        nc.vector.tensor_copy(ts_slots[:], ts_row[:].indirect(offsets[:]))
-        ts_turned = psum_t.tile([P, PACK, P], F32, name="ts_turned", tag="turned")
-        for i in range(PACK):
-            nc.tensor.transpose(ts_turned[:, i, :], ts_slots[:, i:SLOTS:PACK], ident32[:])
-        ts_column = keep.tile([P, PACK], F32, name="ts_column")
-        nc.scalar.copy(ts_column[:], ts_turned[:, :, 0])
-        ts_spread = psum_t.tile([P, SLOTS], F32, name="ts_spread", tag="turned")
-        for i in range(PACK):
-            nc.tensor.transpose(ts_spread[:, i * P : (i + 1) * P], ts_column[:, i : i + 1].to_broadcast([P, P]), ident32[:])
-        ts_all = keep.tile([P, SLOTS], F32, name="ts_all")
-        nc.scalar.copy(ts_all[:], ts_spread[:])
-
-        gather_plane(2)
-
-        def gather_last(h):
-            nc.vector.tensor_copy(
-                k_quads[:, h * HALF : (h + 1) * HALF, 3],
-                planes[3].indirect(offsets[:, h * HALF // 16 : (h + 1) * HALF // 16]),
-            )
-
-        gather_last(0)
-        gather_last(1)
-        for b in range(BLOCKS):
-            rows = slice(b * P, (b + 1) * P)
-            nc.scalar.copy(q_quads[:, rows, :], q_raw[:, :, rows].rearrange("p j q -> p q j"))
-        scores, total, prob = [], [], []
-        for b in range(BLOCKS):
-            scores.append(psum.tile([P, SLOTS], F32, name=f"scores{b}"))
-            total.append(keep.tile([P, 1], F32, name=f"total{b}"))
-            prob.append(keep.tile([P, PACK, P], F32, name=f"prob{b}"))
-        for h in range(2):
-            quantize(k_codes, k_scales, k_quads, h * HALF, (h + 1) * HALF)
-        for b in range(BLOCKS):
-            rows = slice(b * P, (b + 1) * P)
-            quantize(q_codes, q_scales, q_quads, b * P, (b + 1) * P)
-            if b == 0:
-                quantize(v_codes, v_scales, v_quads, 0, 2 * P)
+        def product(result, stationary, moving):
             nc.tensor.matmul_mx(
-                out=scores[b][:],
-                lhsT=q_codes[:, rows].bitcast(FP8X4),
-                lhsT_scale=q_scales[:, rows],
-                rhs=k_codes[:].bitcast(FP8X4),
-                rhs_scale=k_scales[:],
+                out=result[:],
+                lhsT=stationary[0][:].bitcast(FP8X4),
+                lhsT_scale=stationary[1][:],
+                rhs=moving[0][:].bitcast(FP8X4),
+                rhs_scale=moving[1][:],
                 start=True,
                 stop=True,
             )
-        scaled, capped, minus_m = [], [], []
-        for b in range(BLOCKS):
-            scaled.append(keep.tile([P, PACK, P], F32, name=f"scaled{b}"))
-            capped.append(keep.tile([P, PACK, P], F32, name=f"capped{b}"))
-            minus_m.append(keep.tile([P, 1], F32, name=f"minus_m{b}"))
-        for b in range(BLOCKS):
-            nc.vector.tensor_tensor(
-                scaled[b][:],
-                scores[b][:].rearrange("q (s i) -> q i s", i=PACK),
-                ts_all[:].rearrange("q (i s) -> q i s", i=PACK),
-                ALU.mult,
+
+        ts_table = shared.tile([P, TOKENS], F32, name="ts_table", align_bytes=64, offset=0)
+        for g in range(per_row // PACK):
+            spread = psum.tile([P, PACK, P], F32, name=f"spread{g}", tag=f"bank{g}")
+            for c in range(PACK):
+                column = g * PACK + c
+                nc.tensor.transpose(spread[:, c, :], ts_rows[:, column : column + 1].to_broadcast([P, P]), ident[:])
+            nc.scalar.copy(
+                ts_table[:].rearrange("q (p c) -> q p c", c=per_row)[:, :, g * PACK : (g + 1) * PACK],
+                spread[:].rearrange("q c p -> q p c"),
             )
-            nc.scalar.activation(capped[b][:], scaled[b][:], ACT.Tanh, scale=1.0 / CAP)
+        v_early = keep.tile([P, 2, P, PACK], BF16, name="v_early", align_bytes=64)
+
+        def gather(t, picked):
+            nc.vector.tensor_copy(picked.rearrange("p u s e -> p s u e"), planes[t][:].indirect(offsets[:]))
+
+        def turn_plane(picked, bank, quads):
+            words = picked.rearrange("p u s e -> p u (s e)").bitcast(F32)
+            turned = psum.tile([P, 2, P], F32, name="turned", tag=bank)
+            for u in range(2):
+                nc.tensor.transpose(turned[:, u, :], words[:, u, :], ident[:])
+            nc.scalar.copy(quads.bitcast(F32), turned[:].rearrange("s u (h p) -> s h p u", h=2))
+
+        def quantize_values(t, quads):
+            for h in range(2):
+                quantize(values[h], quads[:, h], t * P // 2)
+
+        k_quads = keep.tile([P, SLOTS, PACK], BF16, name="k_quads", align_bytes=64)
+        k_places = k_quads[:].rearrange("p (h u c) t -> p h u c t", h=2, u=2)
+        third = keep.tile([P, 2, P, 2], BF16, name="third")
+        v_third = keep.tile([P, 2, P // 2, PACK], BF16, name="v_third", align_bytes=64)
+        gather(2, third[:])
+        nc.vector.tensor_copy(k_places[:, :, :, :, 2], third[:].rearrange("p u (h s) e -> p h u (s e)", h=2))
+        turn_plane(third[:], "bank3", v_third[:])
+
+        ts_slots = keep.tile([P, SLOTS], F32, name="ts_slots")
+        nc.vector.tensor_copy(ts_slots[:], ts_table[:].indirect(offsets[:]))
+        ts_dealt = keep.tile([P, 2, PACK, P // 2], F32, name="ts_dealt")
+        nc.scalar.copy(ts_dealt[:], ts_slots[:].rearrange("q (h s i) -> q h i s", h=2, i=PACK))
+        ts_turned = psum.tile([P, PACK, P], F32, name="ts_turned", tag="bank0")
+        for i in range(PACK):
+            nc.tensor.transpose(ts_turned[:, i, :], ts_slots[:, i:SLOTS:PACK], ident[:])
+        ts_column = keep.tile([P, PACK], F32, name="ts_column")
+        nc.scalar.copy(ts_column[:], ts_turned[:, :, 0])
+
+        early = shared.tile([P, 2, 2, P, 2], BF16, name="early", align_bytes=64, offset=0)
+        for t in range(2):
+            gather(t, early[:, t])
+        for h, copy in enumerate((nc.scalar.copy, nc.vector.tensor_copy)):
+            copy(k_places[:, h, :, :, 0:2], early[:].rearrange("p t u (h s) e -> p h u (s e) t", h=2)[:, h])
+        for t in range(2):
+            turn_plane(early[:, t], f"bank{2 - t}", v_early[:, :, t * P // 2 : (t + 1) * P // 2])
+        for h, window in enumerate((planes[3][:, :PREFIX], planes[3][:])):
+            nc.vector.tensor_copy(
+                k_places[:, h, :, :, 3].rearrange("p u (s e) -> p s u e", e=2),
+                window.indirect(offsets[:, h * HALF // 16 : (h + 1) * HALF // 16]),
+            )
+
+        def weave_queries(b):
+            q_quads = shared.tile([P, P, PACK], BF16, name=f"q_quads{b}", align_bytes=64, offset=1024 * b)
+            nc.scalar.copy(q_quads[:], q_raw[b][:].rearrange("p j q -> p q j"))
+            return q_quads
+
+        q_quads = weave_queries(0)
+        last = keep.tile([P, 2, P, 2], BF16, name="last", tag="q_raw0", align_bytes=64)
+        nc.scalar.copy(
+            last[:].rearrange("p u (h s) e -> p u h (s e)", h=2), k_places[:, :, :, :, 3].rearrange("p h u c -> p u h c")
+        )
+        keys = [operand("k0", HALF, "plane3"), operand("k1", HALF)]
+        queries = [operand(f"q{b}", P) for b in range(BLOCKS)]
+        quantize(keys[0], k_quads[:, :HALF])
+        quantize(queries[0], q_quads[:])
+        quantize(keys[1], k_quads[:, HALF:])
+        values = []
+        for h in range(2):
+            codes = keep.tile([P, HALF], U32, name=f"v{h}_codes", align_bytes=64)
+            scales = shared.tile([P, HALF], U8, name=f"v{h}_scales", align_bytes=64, offset=HALF * h)
+            values.append((codes, scales))
+        q_quads = weave_queries(1)
+        quantize(queries[1], q_quads[:])
+        scores = [[None, None] for b in range(BLOCKS)]
         for b in range(BLOCKS):
+            for h in range(2):
+                scores[b][h] = psum.tile([P, HALF], F32, name=f"scores{b}{h}", tag=f"bank{2 * b + h}")
+                product(scores[b][h], queries[b], keys[h])
+        v_last = keep.tile([P, 2, P // 2, PACK], BF16, name="v_last", align_bytes=64)
+        turn_plane(last[:], "spare", v_last[:])
+        quantize_values(0, v_early)
+        quantize_values(2, v_third)
+        quantize_values(3, v_last)
+
+        prob, total = [], []
+        for b in range(BLOCKS):
+            scaled = keep.tile([P, 2, PACK, P // 2], F32, name=f"scaled{b}")
+            capped = keep.tile([P, 2, PACK, P // 2], F32, name=f"capped{b}")
+            for h in range(2):
+                nc.vector.tensor_tensor(
+                    scaled[:, h].rearrange("q (u e) s -> q u e s", u=2),
+                    scores[b][h][:].rearrange("q (u s e) -> q u e s", u=2, e=2),
+                    ts_dealt[:, h].rearrange("q (u e) s -> q u e s", u=2),
+                    ALU.mult,
+                )
+                nc.scalar.activation(capped[:, h], scaled[:, h], ACT.Tanh, scale=1.0 / CAP)
             top = keep.tile([P, 1], F32, name=f"top{b}")
-            nc.vector.tensor_reduce(top[:], scaled[b][:].rearrange("q i s -> q (i s)"), AX.X, ALU.max)
+            nc.vector.tensor_reduce(top[:], scaled[:].rearrange("q h i s -> q (h i s)"), AX.X, ALU.max)
             pair = keep.tile([P, 2], F32, name=f"pair{b}")
+            minus_m = keep.tile([P, 1], F32, name=f"minus_m{b}")
             nc.scalar.activation(
-                pair[:], top[:].to_broadcast([P, 2]), ACT.Tanh, scale=-1.0 / CAP, accum_out=minus_m[b][:]
+                pair[:], top[:].to_broadcast([P, 2]), ACT.Tanh, scale=-1.0 / CAP, accum_out=minus_m[:]
             )
+            prob.append(keep.tile([P, PACK, P], F32, name=f"prob{b}"))
+            total.append(keep.tile([P, 1], F32, name=f"total{b}"))
             nc.scalar.activation(
-                prob[b][:], capped[b][:], ACT.Exp, bias=minus_m[b][:], scale=CAP, accum_out=total[b][:]
+                prob[b][:].rearrange("q i (h s) -> q h i s", h=2),
+                capped[:],
+                ACT.Exp,
+                bias=minus_m[:],
+                scale=CAP,
+                accum_out=total[b][:],
             )
-        for t in range(2, PACK):
-            turn_plane(t, nc.vector.tensor_copy, psum.tile([P, PACK, P], BF16, name=f"turned{t}", tag=f"scores{t - 2}"))
-        turned_prob = []
+        y = [[None, None] for b in range(BLOCKS)]
         for b in range(BLOCKS):
-            turned_prob.append(psum.tile([P, PACK, P], F32, name=f"turned_prob{b}"))
+            turned_prob = psum.tile([P, PACK, P], F32, name=f"turned_prob{b}")
             for i in range(PACK):
-                nc.tensor.transpose(turned_prob[b][:, i, :], prob[b][:, i, :], ident32[:])
-        quantize(v_codes, v_scales, v_quads, 2 * P, 3 * P)
-        for b in range(BLOCKS):
+                nc.tensor.transpose(turned_prob[:, i, :], prob[b][:, i, :], ident[:])
+            w_quads = keep.tile([P, P, PACK], BF16, name=f"w_quads{b}", align_bytes=64)
             nc.vector.tensor_tensor(
-                w_quads[:, b * P : (b + 1) * P, :],
-                turned_prob[b][:].rearrange("s i q -> s q i"),
+                w_quads[:],
+                turned_prob[:].rearrange("s i q -> s q i"),
                 ts_column[:].unsqueeze(1).to_broadcast([P, P, PACK]),
                 ALU.mult,
             )
-        quantize(v_codes, v_scales, v_quads, 3 * P, 4 * P)
-        y = []
-        for b in range(BLOCKS):
-            rows = slice(b * P, (b + 1) * P)
-            quantize(w_codes, w_scales, w_quads, b * P, (b + 1) * P)
-            y.append(psum.tile([P, FEATURES], F32, name=f"y{b}"))
-            nc.tensor.matmul_mx(
-                out=y[b][:],
-                lhsT=w_codes[:, rows].bitcast(FP8X4),
-                lhsT_scale=w_scales[:, rows],
-                rhs=v_codes[:].bitcast(FP8X4),
-                rhs_scale=v_scales[:],
-                start=True,
-                stop=True,
-            )
+            weights = operand(f"w{b}", P)
+            quantize(weights, w_quads[:])
+            for h in range(2):
+                y[b][h] = psum.tile([P, HALF], F32, name=f"y{b}{h}", tag=f"bank{2 * b + h}")
+                product(y[b][h], weights, values[h])
         for b in range(BLOCKS):
             rows = slice(b * P, (b + 1) * P)
             inverse = keep.tile([P, 1], F32, name=f"inverse{b}")
             nc.vector.reciprocal(inverse[:], total[b][:])
-            result = keep.tile([P, P, PACK], F32, name=f"result{b}")
-            pieces = 1 if b == 0 else 2
-            for piece in range(pieces):
-                part = slice(piece * P // pieces, (piece + 1) * P // pieces)
+            for h in range(2):
+                columns = slice(h * HALF, (h + 1) * HALF)
+                result = keep.tile([P, HALF], F32, name=f"result{b}{h}")
                 nc.vector.scalar_tensor_tensor(
-                    result[:, part, :],
-                    y[b][:].rearrange("q (t p) -> q p t", t=PACK)[:, part, :],
+                    result[:].rearrange("q (p t) -> q p t", t=PACK),
+                    y[b][h][:].rearrange("q (t p) -> q p t", t=PACK),
                     inverse[:],
-                    channel[:].rearrange("q (p t) -> q p t", t=PACK)[:, part, :],
+                    channel[:, columns].rearrange("q (p t) -> q p t", t=PACK),
                     ALU.mult,
                     ALU.mult,
                 )
-                nc.sync.dma_start(out[0, rows, :].rearrange("q (p t) -> q p t", t=PACK)[:, part, :], result[:, part, :])
+                nc.sync.dma_start(out[0, rows, columns], result[:])

@@ -157,11 +157,6 @@ def tile_attend_x_mla_cap_srt_kernel(tc, qT, cT, ts, ch, offs, out):
         quantize(keys[0], k_quads[:, :HALF])
         quantize(queries[0], q_quads[:])
         quantize(keys[1], k_quads[:, HALF:])
-        values = []
-        for h in range(2):
-            codes = keep.tile([P, HALF], U32, name=f"v{h}_codes", align_bytes=64)
-            scales = shared.tile([P, HALF], U8, name=f"v{h}_scales", align_bytes=64, offset=HALF * h)
-            values.append((codes, scales))
         q_quads = weave_queries(1)
         quantize(queries[1], q_quads[:])
         scores = [[None, None] for b in range(BLOCKS)]
@@ -171,13 +166,10 @@ def tile_attend_x_mla_cap_srt_kernel(tc, qT, cT, ts, ch, offs, out):
                 product(scores[b][h], queries[b], keys[h])
         v_last = keep.tile([P, 2, P // 2, PACK], BF16, name="v_last", align_bytes=64)
         turn_plane(last[:], "spare", v_last[:])
-        quantize_values(0, v_early)
-        quantize_values(2, v_third)
-        quantize_values(3, v_last)
 
         prob, total = [], []
         for b in range(BLOCKS):
-            scaled = keep.tile([P, 2, PACK, P // 2], F32, name=f"scaled{b}")
+            scaled = shared.tile([P, 2, PACK, P // 2], F32, name=f"scaled{b}", align_bytes=64, offset=8192 + 2048 * b)
             capped = keep.tile([P, 2, PACK, P // 2], F32, name=f"capped{b}")
             for h in range(2):
                 nc.vector.tensor_tensor(
@@ -187,53 +179,70 @@ def tile_attend_x_mla_cap_srt_kernel(tc, qT, cT, ts, ch, offs, out):
                     ALU.mult,
                 )
                 nc.scalar.activation(capped[:, h], scaled[:, h], ACT.Tanh, scale=1.0 / CAP)
-            top = keep.tile([P, 1], F32, name=f"top{b}")
-            nc.vector.tensor_reduce(top[:], scaled[:].rearrange("q h i s -> q (h i s)"), AX.X, ALU.max)
-            pair = keep.tile([P, 2], F32, name=f"pair{b}")
+            minus_c = keep.tile([P, 2, PACK, P // 2], F32, name=f"minus_c{b}")
             minus_m = keep.tile([P, 1], F32, name=f"minus_m{b}")
-            nc.scalar.activation(
-                pair[:], top[:].to_broadcast([P, 2]), ACT.Tanh, scale=-1.0 / CAP, accum_out=minus_m[:]
-            )
-            prob.append(keep.tile([P, PACK, P], F32, name=f"prob{b}"))
-            total.append(keep.tile([P, 1], F32, name=f"total{b}"))
-            nc.scalar.activation(
-                prob[b][:].rearrange("q i (h s) -> q h i s", h=2),
-                capped[:],
-                ACT.Exp,
-                bias=minus_m[:],
-                scale=CAP,
-                accum_out=total[b][:],
-            )
+            nc.vector.tensor_scalar(minus_c[:], capped[:], -CAP, None, ALU.mult, ALU.min, accum_out=minus_m[:])
+            prob.append(keep.tile([P, PACK, P], F32, name=f"prob{b}", align_bytes=64))
+            total.append(keep.tile([P, 2], F32, name=f"total{b}"))
+            for u in range(2):
+                nc.scalar.activation(
+                    prob[b][:, 2 * u : 2 * u + 2].rearrange("q i (h s) -> q h i s", h=2),
+                    minus_c[:, :, 2 * u : 2 * u + 2],
+                    ACT.Exp,
+                    bias=minus_m[:],
+                    scale=-1.0,
+                    accum_out=total[b][:, u : u + 1],
+                )
+        values = []
+        for h in range(2):
+            codes = keep.tile([P, HALF], U32, name=f"v{h}_codes", align_bytes=64)
+            scales = shared.tile([P, HALF], U8, name=f"v{h}_scales", align_bytes=64, offset=10240 + HALF * h)
+            values.append((codes, scales))
+        quantize_values(0, v_early)
+        quantize_values(2, v_third)
+        quantize_values(3, v_last)
         y = [[None, None] for b in range(BLOCKS)]
+        turned = []
         for b in range(BLOCKS):
-            turned_prob = psum.tile([P, PACK, P], F32, name=f"turned_prob{b}")
+            turned.append(psum.tile([P, PACK, P], F32, name=f"turned_prob{b}"))
             for i in range(PACK):
-                nc.tensor.transpose(turned_prob[:, i, :], prob[b][:, i, :], ident[:])
-            w_quads = keep.tile([P, P, PACK], BF16, name=f"w_quads{b}", align_bytes=64)
-            nc.vector.tensor_tensor(
-                w_quads[:],
-                turned_prob[:].rearrange("s i q -> s q i"),
-                ts_column[:].unsqueeze(1).to_broadcast([P, P, PACK]),
-                ALU.mult,
-            )
-            weights = operand(f"w{b}", P)
-            quantize(weights, w_quads[:])
+                nc.tensor.transpose(turned[b][:, i, :], prob[b][:, i, :], ident[:])
+        for b in range(BLOCKS):
+            turned_prob = turned[b]
+            weights = operand(f"w{b}", P, "prob1" if b == 0 else None)
+            width = P // (b + 1)
+            pieces = []
+            for lo in range(0, P, width):
+                tag = "w_quads_first" if (b, lo) == (1, 0) else "w_quads"
+                w_quads = keep.tile([P, width, PACK], BF16, name=f"w_quads{b}{lo}", tag=tag, align_bytes=64)
+                nc.vector.tensor_tensor(
+                    w_quads[:],
+                    turned_prob[:].rearrange("s i q -> s q i")[:, lo : lo + width],
+                    ts_column[:].unsqueeze(1).to_broadcast([P, width, PACK]),
+                    ALU.mult,
+                )
+                pieces.append(w_quads)
+            for n, w_quads in enumerate(pieces):
+                quantize(weights, w_quads[:], n * width)
             for h in range(2):
                 y[b][h] = psum.tile([P, HALF], F32, name=f"y{b}{h}", tag=f"bank{2 * b + h}")
                 product(y[b][h], weights, values[h])
         for b in range(BLOCKS):
             rows = slice(b * P, (b + 1) * P)
             inverse = keep.tile([P, 1], F32, name=f"inverse{b}")
-            nc.vector.reciprocal(inverse[:], total[b][:])
+            row_sum = keep.tile([P, 1], F32, name=f"row_sum{b}")
+            nc.vector.tensor_tensor(row_sum[:], total[b][:, 0:1], total[b][:, 1:2], ALU.add)
+            nc.vector.reciprocal(inverse[:], row_sum[:])
+            tag = "w_quads" if b == 0 else "last_result"
+            result = keep.tile([P, FEATURES], F32, name=f"result{b}", tag=tag, align_bytes=64)
             for h in range(2):
                 columns = slice(h * HALF, (h + 1) * HALF)
-                result = keep.tile([P, HALF], F32, name=f"result{b}{h}")
                 nc.vector.scalar_tensor_tensor(
-                    result[:].rearrange("q (p t) -> q p t", t=PACK),
+                    result[:, columns].rearrange("q (p t) -> q p t", t=PACK),
                     y[b][h][:].rearrange("q (t p) -> q p t", t=PACK),
                     inverse[:],
                     channel[:, columns].rearrange("q (p t) -> q p t", t=PACK),
                     ALU.mult,
                     ALU.mult,
                 )
-                nc.sync.dma_start(out[0, rows, columns], result[:])
+                nc.sync.dma_start(out[0, rows, columns], result[:, columns])

@@ -111,34 +111,35 @@ def tile_attend_x_mla_cap_srt_kernel(tc, qT, cT, ts, ch, offs, out):
             for h in range(2):
                 quantize(values[h], quads[:, h], t * P // 2)
 
-        k_quads = keep.tile([P, SLOTS, PACK], BF16, name="k_quads", align_bytes=64)
-        k_places = k_quads[:].rearrange("p (h u c) t -> p h u c t", h=2, u=2)
+        k_quads = [keep.tile([P, HALF, PACK], BF16, name=f"k_quads{h}", align_bytes=64) for h in range(2)]
+        k_places = [k_quads[h][:].rearrange("p (u c) t -> p u c t", u=2) for h in range(2)]
         third = keep.tile([P, 2, P, 2], BF16, name="third")
         v_third = keep.tile([P, 2, P // 2, PACK], BF16, name="v_third", align_bytes=64)
         gather(2, third[:])
-        nc.vector.tensor_copy(k_places[:, :, :, :, 2], third[:].rearrange("p u (h s) e -> p h u (s e)", h=2))
+        for h in range(2):
+            nc.vector.tensor_copy(k_places[h][:, :, :, 2], third[:].rearrange("p u (h s) e -> p h u (s e)", h=2)[:, h])
         turn_plane(third[:], "bank3", v_third[:])
 
-        ts_slots = keep.tile([P, SLOTS], F32, name="ts_slots")
-        nc.vector.tensor_copy(ts_slots[:], ts_table[:].indirect(offsets[:]))
-        ts_dealt = keep.tile([P, 2, PACK, P // 2], F32, name="ts_dealt")
-        nc.scalar.copy(ts_dealt[:], ts_slots[:].rearrange("q (h s i) -> q h i s", h=2, i=PACK))
+        ts_dealt = keep.tile([P, PACK, P], F32, name="ts_dealt")
+        nc.vector.tensor_copy(
+            ts_dealt[:].bitcast(U32).rearrange("q i s -> q s i"), ts_table[:].bitcast(U32).indirect(offsets[:])
+        )
         ts_turned = psum.tile([P, PACK, P], F32, name="ts_turned", tag="bank0")
         for i in range(PACK):
-            nc.tensor.transpose(ts_turned[:, i, :], ts_slots[:, i:SLOTS:PACK], ident[:])
+            nc.tensor.transpose(ts_turned[:, i, :], ts_dealt[:, i, :], ident[:])
         ts_column = keep.tile([P, PACK], F32, name="ts_column")
         nc.scalar.copy(ts_column[:], ts_turned[:, :, 0])
 
         early = shared.tile([P, 2, 2, P, 2], BF16, name="early", align_bytes=64, offset=0)
         for t in range(2):
             gather(t, early[:, t])
-        for h, copy in enumerate((nc.scalar.copy, nc.vector.tensor_copy)):
-            copy(k_places[:, h, :, :, 0:2], early[:].rearrange("p t u (h s) e -> p h u (s e) t", h=2)[:, h])
+        for h, copy in enumerate((nc.vector.tensor_copy, nc.scalar.copy)):
+            copy(k_places[h][:, :, :, 0:2], early[:].rearrange("p t u (h s) e -> p h u (s e) t", h=2)[:, h])
         for t in range(2):
             turn_plane(early[:, t], f"bank{2 - t}", v_early[:, :, t * P // 2 : (t + 1) * P // 2])
         for h, window in enumerate((planes[3][:, :PREFIX], planes[3][:])):
             nc.vector.tensor_copy(
-                k_places[:, h, :, :, 3].rearrange("p u (s e) -> p s u e", e=2),
+                k_places[h][:, :, :, 3].rearrange("p u (s e) -> p s u e", e=2),
                 window.indirect(offsets[:, h * HALF // 16 : (h + 1) * HALF // 16]),
             )
 
@@ -148,24 +149,21 @@ def tile_attend_x_mla_cap_srt_kernel(tc, qT, cT, ts, ch, offs, out):
             return q_quads
 
         q_quads = weave_queries(0)
-        last = keep.tile([P, 2, P, 2], BF16, name="last", tag="q_raw0", align_bytes=64)
-        nc.scalar.copy(
-            last[:].rearrange("p u (h s) e -> p u h (s e)", h=2), k_places[:, :, :, :, 3].rearrange("p h u c -> p u h c")
-        )
         keys = [operand("k0", HALF, "plane3"), operand("k1", HALF)]
         queries = [operand(f"q{b}", P) for b in range(BLOCKS)]
-        quantize(keys[0], k_quads[:, :HALF])
+        quantize(keys[0], k_quads[0][:])
         quantize(queries[0], q_quads[:])
-        quantize(keys[1], k_quads[:, HALF:])
+        quantize(keys[1], k_quads[1][:])
         q_quads = weave_queries(1)
         quantize(queries[1], q_quads[:])
+        last = keep.tile([P, 2, P, 2], BF16, name="last", tag="q_raw1", align_bytes=64)
+        for h in range(2):
+            nc.scalar.copy(last[:].rearrange("p u (h s) e -> p h u (s e)", h=2)[:, h], k_places[h][:, :, :, 3])
         scores = [[None, None] for b in range(BLOCKS)]
         for b in range(BLOCKS):
             for h in range(2):
                 scores[b][h] = psum.tile([P, HALF], F32, name=f"scores{b}{h}", tag=f"bank{2 * b + h}")
                 product(scores[b][h], queries[b], keys[h])
-        v_last = keep.tile([P, 2, P // 2, PACK], BF16, name="v_last", align_bytes=64)
-        turn_plane(last[:], "spare", v_last[:])
 
         prob, total = [], []
         for b in range(BLOCKS):
@@ -175,7 +173,7 @@ def tile_attend_x_mla_cap_srt_kernel(tc, qT, cT, ts, ch, offs, out):
                 nc.vector.tensor_tensor(
                     scaled[:, h].rearrange("q (u e) s -> q u e s", u=2),
                     scores[b][h][:].rearrange("q (u s e) -> q u e s", u=2, e=2),
-                    ts_dealt[:, h].rearrange("q (u e) s -> q u e s", u=2),
+                    ts_dealt[:].rearrange("q (u e) (h s) -> q h u e s", u=2, h=2)[:, h],
                     ALU.mult,
                 )
                 nc.scalar.activation(capped[:, h], scaled[:, h], ACT.Tanh, scale=1.0 / CAP)
@@ -193,6 +191,8 @@ def tile_attend_x_mla_cap_srt_kernel(tc, qT, cT, ts, ch, offs, out):
                     scale=-1.0,
                     accum_out=total[b][:, u : u + 1],
                 )
+        v_last = shared.tile([P, 2, P // 2, PACK], BF16, name="v_last", align_bytes=64, offset=11264)
+        turn_plane(last[:], "spare", v_last[:])
         values = []
         for h in range(2):
             codes = keep.tile([P, HALF], U32, name=f"v{h}_codes", align_bytes=64)

@@ -137,11 +137,14 @@ def tile_attend_x_mla_cap_srt_kernel(tc, qT, cT, ts, ch, offs, out):
             copy(k_places[h][:, :, :, 0:2], early[:].rearrange("p t u (h s) e -> p h u (s e) t", h=2)[:, h])
         for t in range(2):
             turn_plane(early[:, t], f"bank{2 - t}", v_early[:, :, t * P // 2 : (t + 1) * P // 2])
+        last = keep.tile([P, 2, P, 2], BF16, name="last", tag="plane1", align_bytes=64)
         for h, window in enumerate((planes[3][:, :PREFIX], planes[3][:])):
             nc.vector.tensor_copy(
-                k_places[h][:, :, :, 3].rearrange("p u (s e) -> p s u e", e=2),
+                last[:].rearrange("p u s e -> p s u e")[:, h * P // 2 : (h + 1) * P // 2],
                 window.indirect(offsets[:, h * HALF // 16 : (h + 1) * HALF // 16]),
             )
+        for h in range(2):
+            nc.vector.tensor_copy(k_places[h][:, :, :, 3], last[:].rearrange("p u (h s) e -> p h u (s e)", h=2)[:, h])
 
         def weave_queries(b):
             q_quads = shared.tile([P, P, PACK], BF16, name=f"q_quads{b}", align_bytes=64, offset=1024 * b)
@@ -156,9 +159,6 @@ def tile_attend_x_mla_cap_srt_kernel(tc, qT, cT, ts, ch, offs, out):
         quantize(keys[1], k_quads[1][:])
         q_quads = weave_queries(1)
         quantize(queries[1], q_quads[:])
-        last = keep.tile([P, 2, P, 2], BF16, name="last", tag="q_raw1", align_bytes=64)
-        for h in range(2):
-            nc.scalar.copy(last[:].rearrange("p u (h s) e -> p h u (s e)", h=2)[:, h], k_places[h][:, :, :, 3])
         scores = [[None, None] for b in range(BLOCKS)]
         for b in range(BLOCKS):
             for h in range(2):

@@ -35,48 +35,51 @@ def tile_attend_x_mla_cap_srt_kernel(tc, qT, cT, ts, ch, offs, out):
         shared = ctx.enter_context(tc.tile_pool(name="shared", bufs=1))
         psum = ctx.enter_context(tc.psum_pool(name="psum", bufs=1))
 
-        per_row = TOKENS // P
-        ts_rows = keep.tile([P, per_row], F32, name="ts_rows")
-        nc.sync.dma_start(ts_rows[:], ts[0].rearrange("(p c) -> p c", c=per_row))
-        plane_rows = cT.rearrange("(p j) w -> j p w", j=PACK)
-        planes = [keep.tile([P, TOKENS], F32, name=f"plane{t}", align_bytes=64) for t in range(PACK)]
-        nc.sync.dma_start(planes[2][:], plane_rows[2])
+        ts_table = keep.tile([P, TOKENS], F32, name="ts_table", align_bytes=64)
+        nc.scalar.dma_start(ts_table[P - 1 : P, :], ts[0:1, :])
         offsets = keep.tile([P, SLOTS // 16], U16, name="offsets")
+        plane_rows = cT.rearrange("(p j) w -> j p w", j=PACK)
+        planes = [
+            shared.tile([P, TOKENS], F32, name=f"plane{j}", align_bytes=64, offset=8192 * (j + 1)) for j in range(PACK)
+        ]
         nc.sync.dma_start(offsets[:], offs)
-        for t in range(2):
-            nc.sync.dma_start(planes[t][:], plane_rows[t])
-        nc.sync.dma_start(planes[3][:, :PREFIX], plane_rows[3][:, :PREFIX])
-        nc.sync.dma_start(planes[3][:, PREFIX:], plane_rows[3][:, PREFIX:])
+        nc.sync.dma_start(planes[0][:], plane_rows[0])
+        for j in (1, 3, 2):
+            nc.sync.dma_start(planes[j][:], plane_rows[j])
         q_rows = qT[0].rearrange("(p j) q -> p j q", j=PACK)
         q_raw = []
         for b in range(BLOCKS):
-            q_raw.append(keep.tile([P, PACK, P], F32, name=f"q_raw{b}", align_bytes=64))
+            q_raw.append(shared.tile([P, PACK, P], F32, name=f"q_raw{b}", align_bytes=64, offset=40960 + 4096 * b))
             nc.sync.dma_start(q_raw[b][:], q_rows[:, :, b * P : (b + 1) * P])
         channel = keep.tile([P, FEATURES], F32, name="channel")
         nc.sync.dma_start(channel[:], ch)
 
+        nc.vector.memset(ts_table[: P - 1, :], 0.0)
         ident = keep.tile([P, P], F32, name="ident")
         make_identity(nc, ident[:])
         warm = keep.tile([P, 1], F32, name="warm")
-        nc.vector.memset(warm[:], 0.0)
+        nc.gpsimd.memset(warm[:], 0.0)
         nc.scalar.activation(warm[:], warm[:], ACT.Exp)
 
-        def operand(name, width, tag=None):
-            codes = keep.tile([P, width], U32, name=f"{name}_codes", tag=tag or f"{name}_codes", align_bytes=64)
-            scales = keep.tile([P, width], U8, name=f"{name}_scales", align_bytes=64)
+        def operand(name, width, codes_at=None, scales_at=None):
+            if codes_at is None:
+                codes = keep.tile([P, width], U32, name=f"{name}_codes", align_bytes=64)
+            else:
+                codes = shared.tile([P, width], U32, name=f"{name}_codes", align_bytes=64, offset=codes_at)
+            if scales_at is None:
+                scales = keep.tile([P, width], U8, name=f"{name}_scales", align_bytes=64)
+            else:
+                scales = shared.tile([P, width], U8, name=f"{name}_scales", align_bytes=64, offset=scales_at)
             return codes, scales
 
-        def quantize(target, quads, lo=0):
-            hi = lo + quads.shape[1]
+        def quantize(target, quads):
             nc.vector.quantize_mx(
-                out=target[0][:, lo:hi].bitcast(FP8X4),
-                scales=target[1][:, lo:hi],
-                in_=quads.rearrange("p n j -> p (n j)"),
+                out=target[0][:].bitcast(FP8X4), scales=target[1][:], in_=quads.rearrange("p n j -> p (n j)")
             )
 
         def product(result, stationary, moving):
             nc.tensor.matmul_mx(
-                out=result[:],
+                out=result,
                 lhsT=stationary[0][:].bitcast(FP8X4),
                 lhsT_scale=stationary[1][:],
                 rhs=moving[0][:].bitcast(FP8X4),
@@ -85,164 +88,149 @@ def tile_attend_x_mla_cap_srt_kernel(tc, qT, cT, ts, ch, offs, out):
                 stop=True,
             )
 
-        ts_table = shared.tile([P, TOKENS], F32, name="ts_table", align_bytes=64, offset=0)
-        for g in range(per_row // PACK):
-            spread = psum.tile([P, PACK, P], F32, name=f"spread{g}", tag=f"bank{g}")
-            for c in range(PACK):
-                column = g * PACK + c
-                nc.tensor.transpose(spread[:, c, :], ts_rows[:, column : column + 1].to_broadcast([P, P]), ident[:])
-            nc.scalar.copy(
-                ts_table[:].rearrange("q (p c) -> q p c", c=per_row)[:, :, g * PACK : (g + 1) * PACK],
-                spread[:].rearrange("q c p -> q p c"),
-            )
-        v_early = keep.tile([P, 2, P, PACK], BF16, name="v_early", align_bytes=64)
+        def gather(j, picked):
+            nc.vector.tensor_copy(picked.rearrange("p u s e -> p s u e"), planes[j][:].indirect(offsets[:]))
 
-        def gather(t, picked):
-            nc.vector.tensor_copy(picked.rearrange("p u s e -> p s u e"), planes[t][:].indirect(offsets[:]))
-
-        def turn_plane(picked, bank, quads):
+        def turn(picked, turned):
             words = picked.rearrange("p u s e -> p u (s e)").bitcast(F32)
-            turned = psum.tile([P, 2, P], F32, name="turned", tag=bank)
             for u in range(2):
                 nc.tensor.transpose(turned[:, u, :], words[:, u, :], ident[:])
-            nc.scalar.copy(quads.bitcast(F32), turned[:].rearrange("s u (h p) -> s h p u", h=2))
 
-        def quantize_values(t, quads):
-            for h in range(2):
-                quantize(values[h], quads[:, h], t * P // 2)
+        def halves(picked):
+            return picked.rearrange("p u (h s) e -> p h u (s e)", h=2)
+
+        ts_picked = keep.tile([P, PACK, P], F32, name="ts_picked")
+        nc.vector.tensor_copy(ts_picked[:].rearrange("p c s -> p (c s)"), ts_table[:].indirect(offsets[:]))
+        ts_turned = psum.tile([P, PACK, P], F32, name="ts_turned", tag="bank_a0")
+        for c in range(PACK):
+            nc.tensor.transpose(ts_turned[:, c, :], ts_picked[:, c, :], ident[:])
+        ts_column = keep.tile([P, PACK], F32, name="ts_column")
+        nc.scalar.copy(ts_column[:], ts_turned[:, :, P - 1])
+        ts_spread = psum.tile([P, PACK, P], F32, name="ts_spread", tag="bank_a1")
+        for c in range(PACK):
+            nc.tensor.transpose(ts_spread[:, c, :], ts_column[:, c : c + 1].to_broadcast([P, P]), ident[:])
+        ts_dealt = keep.tile([P, 2, P, 2], F32, name="ts_dealt")
+        nc.scalar.copy(ts_dealt[:], ts_spread[:].rearrange("q c (s u e) -> q u (c s) e", u=2, e=2))
 
         k_quads = [keep.tile([P, HALF, PACK], BF16, name=f"k_quads{h}", align_bytes=64) for h in range(2)]
         k_places = [k_quads[h][:].rearrange("p (u c) t -> p u c t", u=2) for h in range(2)]
-        third = keep.tile([P, 2, P, 2], BF16, name="third")
-        v_third = keep.tile([P, 2, P // 2, PACK], BF16, name="v_third", align_bytes=64)
-        gather(2, third[:])
+        first = keep.tile([P, 2, P, 2], BF16, name="first", align_bytes=64)
+        gather(0, first[:])
         for h in range(2):
-            nc.vector.tensor_copy(k_places[h][:, :, :, 2], third[:].rearrange("p u (h s) e -> p h u (s e)", h=2)[:, h])
-        turn_plane(third[:], "bank3", v_third[:])
-
-        ts_dealt = keep.tile([P, PACK, P], F32, name="ts_dealt")
-        nc.vector.tensor_copy(
-            ts_dealt[:].bitcast(U32).rearrange("q i s -> q s i"), ts_table[:].bitcast(U32).indirect(offsets[:])
+            nc.vector.tensor_copy(k_places[h][:, :, :, 0], halves(first[:])[:, h])
+        turned_early = psum.tile([P, 2, 2, P], F32, name="turned_early", tag="bank_a2")
+        turn(first[:], turned_early[:, 0])
+        pair = shared.tile([P, 2, 2, P, 2], BF16, name="pair", align_bytes=64, offset=0)
+        gather(1, pair[:, 0])
+        turn(pair[:, 0], turned_early[:, 1])
+        v_early = keep.tile([P, 2, P, PACK], BF16, name="v_early", align_bytes=64)
+        nc.scalar.copy(
+            v_early[:].bitcast(F32).rearrange("s h (t p) u -> s h t p u", t=2),
+            turned_early[:].rearrange("s t u (h p) -> s h t p u", h=2),
         )
-        ts_turned = psum.tile([P, PACK, P], F32, name="ts_turned", tag="bank0")
-        for i in range(PACK):
-            nc.tensor.transpose(ts_turned[:, i, :], ts_dealt[:, i, :], ident[:])
-        ts_column = keep.tile([P, PACK], F32, name="ts_column")
-        nc.scalar.copy(ts_column[:], ts_turned[:, :, 0])
-
-        early = shared.tile([P, 2, 2, P, 2], BF16, name="early", align_bytes=64, offset=0)
-        for t in range(2):
-            gather(t, early[:, t])
+        gather(3, pair[:, 1])
+        turned_late = psum.tile([P, 2, 2, P], F32, name="turned_late", tag="bank_a3")
+        turn(pair[:, 1], turned_late[:, 1])
         for h, copy in enumerate((nc.vector.tensor_copy, nc.scalar.copy)):
-            copy(k_places[h][:, :, :, 0:2], early[:].rearrange("p t u (h s) e -> p h u (s e) t", h=2)[:, h])
-        for t in range(2):
-            turn_plane(early[:, t], f"bank{2 - t}", v_early[:, :, t * P // 2 : (t + 1) * P // 2])
-        last = keep.tile([P, 2, P, 2], BF16, name="last", tag="plane1", align_bytes=64)
-        for h, window in enumerate((planes[3][:, :PREFIX], planes[3][:])):
+            copy(k_places[h][:, :, :, 2:4], pair[:].rearrange("p t u (h s) e -> p h u (s e) t", h=2)[:, h])
+        last = keep.tile([P, 2, P, 2], BF16, name="last", align_bytes=64)
+        for h in range(2):
             nc.vector.tensor_copy(
                 last[:].rearrange("p u s e -> p s u e")[:, h * P // 2 : (h + 1) * P // 2],
-                window.indirect(offsets[:, h * HALF // 16 : (h + 1) * HALF // 16]),
+                planes[2][:].indirect(offsets[:, h * HALF // 16 : (h + 1) * HALF // 16]),
             )
         for h in range(2):
-            nc.vector.tensor_copy(k_places[h][:, :, :, 3], last[:].rearrange("p u (h s) e -> p h u (s e)", h=2)[:, h])
+            nc.vector.tensor_copy(k_places[h][:, :, :, 1], halves(last[:])[:, h])
+        turn(last[:], turned_late[:, 0])
 
-        def weave_queries(b):
-            q_quads = shared.tile([P, P, PACK], BF16, name=f"q_quads{b}", align_bytes=64, offset=1024 * b)
-            nc.scalar.copy(q_quads[:], q_raw[b][:].rearrange("p j q -> p q j"))
-            return q_quads
-
-        q_quads = weave_queries(0)
-        keys = [operand("k0", HALF, "plane3"), operand("k1", HALF)]
-        queries = [operand(f"q{b}", P) for b in range(BLOCKS)]
-        quantize(keys[0], k_quads[0][:])
-        quantize(queries[0], q_quads[:])
-        quantize(keys[1], k_quads[1][:])
-        q_quads = weave_queries(1)
-        quantize(queries[1], q_quads[:])
-        scores = [[None, None] for b in range(BLOCKS)]
+        q_quads = []
         for b in range(BLOCKS):
-            for h in range(2):
-                scores[b][h] = psum.tile([P, HALF], F32, name=f"scores{b}{h}", tag=f"bank{2 * b + h}")
-                product(scores[b][h], queries[b], keys[h])
-
-        prob, total = [], []
-        for b in range(BLOCKS):
-            scaled = shared.tile([P, 2, PACK, P // 2], F32, name=f"scaled{b}", align_bytes=64, offset=8192 + 2048 * b)
-            capped = keep.tile([P, 2, PACK, P // 2], F32, name=f"capped{b}")
-            for h in range(2):
-                nc.vector.tensor_tensor(
-                    scaled[:, h].rearrange("q (u e) s -> q u e s", u=2),
-                    scores[b][h][:].rearrange("q (u s e) -> q u e s", u=2, e=2),
-                    ts_dealt[:].rearrange("q (u e) (h s) -> q h u e s", u=2, h=2)[:, h],
-                    ALU.mult,
-                )
-                nc.scalar.activation(capped[:, h], scaled[:, h], ACT.Tanh, scale=1.0 / CAP)
-            minus_c = keep.tile([P, 2, PACK, P // 2], F32, name=f"minus_c{b}")
-            minus_m = keep.tile([P, 1], F32, name=f"minus_m{b}")
-            nc.vector.tensor_scalar(minus_c[:], capped[:], -CAP, None, ALU.mult, ALU.min, accum_out=minus_m[:])
-            prob.append(keep.tile([P, PACK, P], F32, name=f"prob{b}", align_bytes=64))
-            total.append(keep.tile([P, 2], F32, name=f"total{b}"))
-            for u in range(2):
-                nc.scalar.activation(
-                    prob[b][:, 2 * u : 2 * u + 2].rearrange("q i (h s) -> q h i s", h=2),
-                    minus_c[:, :, 2 * u : 2 * u + 2],
-                    ACT.Exp,
-                    bias=minus_m[:],
-                    scale=-1.0,
-                    accum_out=total[b][:, u : u + 1],
-                )
-        v_last = shared.tile([P, 2, P // 2, PACK], BF16, name="v_last", align_bytes=64, offset=11264)
-        turn_plane(last[:], "spare", v_last[:])
-        values = []
+            q_quads.append(shared.tile([P, P, PACK], BF16, name=f"q_quads{b}", align_bytes=64, offset=1024 * b))
+            nc.scalar.copy(
+                q_quads[b][:].rearrange("p q (w e) -> p q w e", w=2), q_raw[b][:].rearrange("p (e w) q -> p q w e", w=2)
+            )
+        v_late = shared.tile([P, 2, P, PACK], BF16, name="v_late", align_bytes=64, offset=45056 - 1536)
+        nc.scalar.copy(
+            v_late[:].bitcast(F32).rearrange("s h (t p) u -> s h t p u", t=2),
+            turned_late[:].rearrange("s t u (h p) -> s h t p u", h=2),
+        )
+        last_plane = 8192 * 3
+        keys = [operand("k0", HALF, last_plane), operand("k1", HALF, 40960)]
+        queries = [operand(f"q{b}", P, last_plane + 1024 * (b + 1)) for b in range(BLOCKS)]
+        for n in range(2):
+            quantize(keys[n], k_quads[n][:])
+            quantize(queries[n], q_quads[n][:])
+        values = [[operand(f"v{h}0", P, scales_at=45568 + P * h)] for h in range(2)]
         for h in range(2):
-            codes = keep.tile([P, HALF], U32, name=f"v{h}_codes", align_bytes=64)
-            scales = shared.tile([P, HALF], U8, name=f"v{h}_scales", align_bytes=64, offset=10240 + HALF * h)
-            values.append((codes, scales))
-        quantize_values(0, v_early)
-        quantize_values(2, v_third)
-        quantize_values(3, v_last)
-        y = [[None, None] for b in range(BLOCKS)]
-        turned = []
+            quantize(values[h][0], v_early[:, h])
+        quarters = [(b, h) for b in range(BLOCKS) for h in range(2)]
+        scores = {}
+        for b, h in quarters:
+            scores[b, h] = psum.tile([P, 2, P], F32, name=f"scores{b}{h}", tag=f"bank_b{b}{h}")
+            product(scores[b, h][:].rearrange("q u c -> q (u c)"), queries[b], keys[h])
+
+        scaled = {}
+        capped = [keep.tile([P, 2, 2, P], F32, name=f"capped{b}") for b in range(BLOCKS)]
+        for b, h in quarters:
+            if (b, h) == (0, 0):
+                scaled[b, h] = shared.tile([P, 2, P], F32, name="scaled00", align_bytes=64, offset=45056 + 1024)
+            else:
+                scaled[b, h] = keep.tile([P, 2, P], F32, name=f"scaled{b}{h}")
+            nc.vector.tensor_tensor(scaled[b, h][:], scores[b, h][:], halves(ts_dealt[:])[:, h], ALU.mult)
+            nc.scalar.activation(capped[b][:, :, h], scaled[b, h][:], ACT.Tanh, scale=1.0 / CAP)
+        minus_c, minus_m = [], []
         for b in range(BLOCKS):
-            turned.append(psum.tile([P, PACK, P], F32, name=f"turned_prob{b}"))
-            for i in range(PACK):
-                nc.tensor.transpose(turned[b][:, i, :], prob[b][:, i, :], ident[:])
+            minus_c.append(keep.tile([P, 2, HALF], F32, name=f"minus_c{b}"))
+            minus_m.append(keep.tile([P, 1], F32, name=f"minus_m{b}"))
+            nc.vector.tensor_scalar(
+                minus_c[b][:],
+                capped[b][:].rearrange("q u h c -> q u (h c)"),
+                -CAP,
+                None,
+                ALU.mult,
+                ALU.min,
+                accum_out=minus_m[b][:],
+            )
+        total = keep.tile([P, BLOCKS, 2], F32, name="total")
+        w_quads = []
         for b in range(BLOCKS):
-            turned_prob = turned[b]
-            weights = operand(f"w{b}", P, "prob1" if b == 0 else None)
-            width = P // (b + 1)
-            pieces = []
-            for lo in range(0, P, width):
-                tag = "w_quads_first" if (b, lo) == (1, 0) else "w_quads"
-                w_quads = keep.tile([P, width, PACK], BF16, name=f"w_quads{b}{lo}", tag=tag, align_bytes=64)
-                nc.vector.tensor_tensor(
-                    w_quads[:],
-                    turned_prob[:].rearrange("s i q -> s q i")[:, lo : lo + width],
-                    ts_column[:].unsqueeze(1).to_broadcast([P, width, PACK]),
-                    ALU.mult,
+            w_turned = psum.tile([P, 2, P], F32, name=f"w_turned{b}", tag=f"bank_a{b}")
+            for u in range(2):
+                prob = shared.tile([P, HALF], F32, name=f"prob{b}{u}", align_bytes=64, offset=2048 + 1024 * (2 * b + u))
+                nc.scalar.activation(
+                    prob[:], minus_c[b][:, u], ACT.Exp, bias=minus_m[b][:], scale=-1.0, accum_out=total[:, b, u : u + 1]
                 )
-                pieces.append(w_quads)
-            for n, w_quads in enumerate(pieces):
-                quantize(weights, w_quads[:], n * width)
-            for h in range(2):
-                y[b][h] = psum.tile([P, HALF], F32, name=f"y{b}{h}", tag=f"bank{2 * b + h}")
-                product(y[b][h], weights, values[h])
-        for b in range(BLOCKS):
-            rows = slice(b * P, (b + 1) * P)
-            inverse = keep.tile([P, 1], F32, name=f"inverse{b}")
-            row_sum = keep.tile([P, 1], F32, name=f"row_sum{b}")
-            nc.vector.tensor_tensor(row_sum[:], total[b][:, 0:1], total[b][:, 1:2], ALU.add)
-            nc.vector.reciprocal(inverse[:], row_sum[:])
-            tag = "w_quads" if b == 0 else "last_result"
-            result = keep.tile([P, FEATURES], F32, name=f"result{b}", tag=tag, align_bytes=64)
-            for h in range(2):
-                columns = slice(h * HALF, (h + 1) * HALF)
-                nc.vector.scalar_tensor_tensor(
-                    result[:, columns].rearrange("q (p t) -> q p t", t=PACK),
-                    y[b][h][:].rearrange("q (t p) -> q p t", t=PACK),
-                    inverse[:],
-                    channel[:, columns].rearrange("q (p t) -> q p t", t=PACK),
-                    ALU.mult,
-                    ALU.mult,
-                )
-                nc.sync.dma_start(out[0, rows, columns], result[:, columns])
+                w_pairs = keep.tile([P, HALF], BF16, name=f"w_pairs{b}{u}", align_bytes=64)
+                nc.vector.tensor_tensor(w_pairs[:], prob[:], ts_dealt[:, u].rearrange("q s e -> q (s e)"), ALU.mult)
+                nc.tensor.transpose(w_turned[:, u, :], w_pairs[:].bitcast(F32), ident[:])
+            w_quads.append((keep.tile([P, P, PACK], BF16, name=f"w_quads{b}", align_bytes=64), w_turned))
+        for quads, w_turned in w_quads:
+            nc.scalar.copy(quads[:].bitcast(F32), w_turned[:].rearrange("s u q -> s q u"))
+        last_prob = 2048 + 1024 * 3
+        for h in range(2):
+            values[h].append(operand(f"v{h}1", P, scales_at=last_prob + P * h))
+            quantize(values[h][1], v_late[:, h])
+        weights = [operand("w0", P, scales_at=last_prob + 4 * P), operand("w1", P)]
+        quantize(weights[0], w_quads[0][0][:])
+        row_sum = keep.tile([P, BLOCKS], F32, name="row_sum")
+        nc.vector.tensor_tensor(row_sum[:], total[:, :, 0], total[:, :, 1], ALU.add)
+        inverse = keep.tile([P, BLOCKS], F32, name="inverse")
+        nc.vector.reciprocal(inverse[:], row_sum[:])
+        quantize(weights[1], w_quads[1][0][:])
+        y = {}
+        for b, h in quarters:
+            y[b, h] = psum.tile([P, 2, P], F32, name=f"y{b}{h}", tag=f"bank_b{b}{h}")
+            for n in range(2):
+                product(y[b, h][:, n, :], weights[b], values[h][n])
+        results = [keep.tile([P, FEATURES], F32, name=f"result{b}", tag=("w_quads1", "result1")[b], align_bytes=64) for b in range(BLOCKS)]
+        for b, h in quarters:
+            columns = slice(h * HALF, (h + 1) * HALF)
+            nc.vector.scalar_tensor_tensor(
+                results[b][:, columns].rearrange("q (p t) -> q p t", t=PACK),
+                y[b, h][:].rearrange("q n (t p) -> q p (n t)", t=2),
+                inverse[:, b : b + 1],
+                channel[:, columns].rearrange("q (p t) -> q p t", t=PACK),
+                ALU.mult,
+                ALU.mult,
+            )
+            nc.sync.dma_start(out[0, b * P : (b + 1) * P, columns], results[b][:, columns])

@@ -118,7 +118,7 @@ def tile_attend_x_mla_cap_srt_kernel(tc, qT, cT, ts, ch, offs, out):
         gather(0, first[:])
         for h in range(2):
             nc.vector.tensor_copy(k_places[h][:, :, :, 0], halves(first[:])[:, h])
-        turned_early = psum.tile([P, 2, 2, P], F32, name="turned_early", tag="bank_a2")
+        turned_early = psum.tile([P, 2, 2, P], F32, name="turned_early", tag="bank_a1")
         turn(first[:], turned_early[:, 0])
         pair = shared.tile([P, 2, 2, P, 2], BF16, name="pair", align_bytes=64, offset=0)
         gather(1, pair[:, 0])
@@ -131,8 +131,10 @@ def tile_attend_x_mla_cap_srt_kernel(tc, qT, cT, ts, ch, offs, out):
         gather(3, pair[:, 1])
         turned_late = psum.tile([P, 2, 2, P], F32, name="turned_late", tag="bank_a3")
         turn(pair[:, 1], turned_late[:, 1])
-        for h, copy in enumerate((nc.vector.tensor_copy, nc.scalar.copy)):
-            copy(k_places[h][:, :, :, 2:4], pair[:].rearrange("p t u (h s) e -> p h u (s e) t", h=2)[:, h])
+        pair_halves = pair[:].rearrange("p t u (h s) e -> p h u (s e) t", h=2)
+        nc.vector.tensor_copy(k_places[0][:, 0, :, 2:4], pair_halves[:, 0, 0])
+        nc.scalar.copy(k_places[0][:, 1, :, 2:4], pair_halves[:, 0, 1])
+        nc.scalar.copy(k_places[1][:, :, :, 2:4], pair_halves[:, 1])
         last = keep.tile([P, 2, P, 2], BF16, name="last", align_bytes=64)
         for h in range(2):
             nc.vector.tensor_copy(
@@ -160,9 +162,8 @@ def tile_attend_x_mla_cap_srt_kernel(tc, qT, cT, ts, ch, offs, out):
         for n in range(2):
             quantize(keys[n], k_quads[n][:])
             quantize(queries[n], q_quads[n][:])
-        values = [[operand(f"v{h}0", P, scales_at=45568 + P * h)] for h in range(2)]
-        for h in range(2):
-            quantize(values[h][0], v_early[:, h])
+        values = [[operand("v00", P, scales_at=45568)], []]
+        quantize(values[0][0], v_early[:, 0])
         quarters = [(b, h) for b in range(BLOCKS) for h in range(2)]
         scores = {}
         for b, h in quarters:
@@ -207,11 +208,13 @@ def tile_attend_x_mla_cap_srt_kernel(tc, qT, cT, ts, ch, offs, out):
         for quads, w_turned in w_quads:
             nc.scalar.copy(quads[:].bitcast(F32), w_turned[:].rearrange("s u q -> s q u"))
         last_prob = 2048 + 1024 * 3
-        for h in range(2):
-            values[h].append(operand(f"v{h}1", P, scales_at=last_prob + P * h))
-            quantize(values[h][1], v_late[:, h])
+        values[0].append(operand("v01", P, scales_at=last_prob))
+        quantize(values[0][1], v_late[:, 0])
+        values[1].extend(operand(f"v1{n}", P, scales_at=last_prob + P * (n + 1)) for n in range(2))
         weights = [operand("w0", P, scales_at=last_prob + 4 * P), operand("w1", P)]
+        quantize(values[1][0], v_early[:, 1])
         quantize(weights[0], w_quads[0][0][:])
+        quantize(values[1][1], v_late[:, 1])
         row_sum = keep.tile([P, BLOCKS], F32, name="row_sum")
         nc.vector.tensor_tensor(row_sum[:], total[:, :, 0], total[:, :, 1], ALU.add)
         inverse = keep.tile([P, BLOCKS], F32, name="inverse")

@@ -123,11 +123,6 @@ def tile_attend_x_mla_cap_srt_kernel(tc, qT, cT, ts, ch, offs, out):
         pair = shared.tile([P, 2, 2, P, 2], BF16, name="pair", align_bytes=64, offset=0)
         gather(1, pair[:, 0])
         turn(pair[:, 0], turned_early[:, 1])
-        v_early = keep.tile([P, 2, P, PACK], BF16, name="v_early", align_bytes=64)
-        nc.scalar.copy(
-            v_early[:].bitcast(F32).rearrange("s h (t p) u -> s h t p u", t=2),
-            turned_early[:].rearrange("s t u (h p) -> s h t p u", h=2),
-        )
         gather(3, pair[:, 1])
         turned_late = psum.tile([P, 2, 2, P], F32, name="turned_late", tag="bank_a3")
         turn(pair[:, 1], turned_late[:, 1])
@@ -151,7 +146,12 @@ def tile_attend_x_mla_cap_srt_kernel(tc, qT, cT, ts, ch, offs, out):
             nc.scalar.copy(
                 q_quads[b][:].rearrange("p q (w e) -> p q w e", w=2), q_raw[b][:].rearrange("p (e w) q -> p q w e", w=2)
             )
-        v_late = shared.tile([P, 2, P, PACK], BF16, name="v_late", align_bytes=64, offset=45056 - 1536)
+        v_early = shared.tile([P, 2, P, PACK], BF16, name="v_early", align_bytes=64, offset=46464)
+        nc.scalar.copy(
+            v_early[:].bitcast(F32).rearrange("s h (t p) u -> s h t p u", t=2),
+            turned_early[:].rearrange("s t u (h p) -> s h t p u", h=2),
+        )
+        v_late = shared.tile([P, 2, P, PACK], BF16, name="v_late", align_bytes=64, offset=43264)
         nc.scalar.copy(
             v_late[:].bitcast(F32).rearrange("s h (t p) u -> s h t p u", t=2),
             turned_late[:].rearrange("s t u (h p) -> s h t p u", h=2),
@@ -162,7 +162,7 @@ def tile_attend_x_mla_cap_srt_kernel(tc, qT, cT, ts, ch, offs, out):
         for n in range(2):
             quantize(keys[n], k_quads[n][:])
             quantize(queries[n], q_quads[n][:])
-        values = [[operand("v00", P, scales_at=45568)], []]
+        values = [[operand("v00", P, scales_at=45312)], []]
         quantize(values[0][0], v_early[:, 0])
         quarters = [(b, h) for b in range(BLOCKS) for h in range(2)]
         scores = {}
@@ -174,7 +174,7 @@ def tile_attend_x_mla_cap_srt_kernel(tc, qT, cT, ts, ch, offs, out):
         capped = [keep.tile([P, 2, 2, P], F32, name=f"capped{b}") for b in range(BLOCKS)]
         for b, h in quarters:
             if (b, h) == (0, 0):
-                scaled[b, h] = shared.tile([P, 2, P], F32, name="scaled00", align_bytes=64, offset=45056 + 1024)
+                scaled[b, h] = shared.tile([P, 2, P], F32, name="scaled00", align_bytes=64, offset=45440)
             else:
                 scaled[b, h] = keep.tile([P, 2, P], F32, name=f"scaled{b}{h}")
             nc.vector.tensor_tensor(scaled[b, h][:], scores[b, h][:], halves(ts_dealt[:])[:, h], ALU.mult)
@@ -216,7 +216,7 @@ def tile_attend_x_mla_cap_srt_kernel(tc, qT, cT, ts, ch, offs, out):
         quantize(weights[0], w_quads[0][0][:])
         quantize(values[1][1], v_late[:, 1])
         row_sum = keep.tile([P, BLOCKS], F32, name="row_sum")
-        nc.vector.tensor_tensor(row_sum[:], total[:, :, 0], total[:, :, 1], ALU.add)
+        nc.gpsimd.tensor_tensor(row_sum[:], total[:, :, 0], total[:, :, 1], ALU.add)
         inverse = keep.tile([P, BLOCKS], F32, name="inverse")
         nc.vector.reciprocal(inverse[:], row_sum[:])
         quantize(weights[1], w_quads[1][0][:])

@@ -11,7 +11,6 @@ U8 = mybir.dt.uint8
 FP8X4 = mybir.dt.float8_e4m3fn_x4
 ACT = mybir.ActivationFunctionType
 ALU = mybir.AluOpType
-AX = mybir.AxisListType
 
 P = 128
 PACK = 4
@@ -21,9 +20,20 @@ QUERIES = 256
 FEATURES = 512
 BLOCKS = QUERIES // P
 HALF = SLOTS // 2
-BANK = 512
-PREFIX = TOKENS - HALF
+LIST_ROWS = 16
 CAP = 2.0
+
+KIB = 1024
+PAIR_AT = 0
+PROB_AT = 2 * KIB
+LAST_PROB_AT = PROB_AT + 3 * KIB
+PLANES_AT = 8 * KIB
+LAST_PLANE_AT = PLANES_AT + 2 * 8 * KIB
+Q_RAW_AT = (40 * KIB, 44 * KIB)
+V_LATE_AT = Q_RAW_AT[1] + 256 - 2 * KIB
+FIRST_V_SCALES_AT = V_LATE_AT + 2 * KIB
+FIRST_SCALED_AT = FIRST_V_SCALES_AT + P
+V_EARLY_AT = FIRST_SCALED_AT + KIB
 
 FLOPS = 2 * 2 * QUERIES * SLOTS * FEATURES
 
@@ -37,19 +47,20 @@ def tile_attend_x_mla_cap_srt_kernel(tc, qT, cT, ts, ch, offs, out):
 
         ts_table = keep.tile([P, TOKENS], F32, name="ts_table", align_bytes=64)
         nc.scalar.dma_start(ts_table[P - 1 : P, :], ts[0:1, :])
-        offsets = keep.tile([P, SLOTS // 16], U16, name="offsets")
+        offsets = keep.tile([P, SLOTS // LIST_ROWS], U16, name="offsets")
         plane_rows = cT.rearrange("(p j) w -> j p w", j=PACK)
         planes = [
-            shared.tile([P, TOKENS], F32, name=f"plane{j}", align_bytes=64, offset=8192 * (j + 1)) for j in range(PACK)
+            shared.tile([P, TOKENS], F32, name=f"plane{j}", align_bytes=64, offset=PLANES_AT + 8 * KIB * j)
+            for j in range(PACK)
         ]
-        nc.sync.dma_start(offsets[:], offs)
         nc.sync.dma_start(planes[0][:], plane_rows[0])
+        nc.sync.dma_start(offsets[:], offs)
         for j in (1, 3, 2):
             nc.sync.dma_start(planes[j][:], plane_rows[j])
         q_rows = qT[0].rearrange("(p j) q -> p j q", j=PACK)
         q_raw = []
         for b in range(BLOCKS):
-            q_raw.append(shared.tile([P, PACK, P], F32, name=f"q_raw{b}", align_bytes=64, offset=40960 + 4096 * b))
+            q_raw.append(shared.tile([P, PACK, P], F32, name=f"q_raw{b}", align_bytes=64, offset=Q_RAW_AT[b]))
             nc.sync.dma_start(q_raw[b][:], q_rows[:, :, b * P : (b + 1) * P])
         channel = keep.tile([P, FEATURES], F32, name="channel")
         nc.sync.dma_start(channel[:], ch)
@@ -61,16 +72,13 @@ def tile_attend_x_mla_cap_srt_kernel(tc, qT, cT, ts, ch, offs, out):
         nc.gpsimd.memset(warm[:], 0.0)
         nc.scalar.activation(warm[:], warm[:], ACT.Exp)
 
+        def place(name, width, dtype, at):
+            if at is None:
+                return keep.tile([P, width], dtype, name=name, align_bytes=64)
+            return shared.tile([P, width], dtype, name=name, align_bytes=64, offset=at)
+
         def operand(name, width, codes_at=None, scales_at=None):
-            if codes_at is None:
-                codes = keep.tile([P, width], U32, name=f"{name}_codes", align_bytes=64)
-            else:
-                codes = shared.tile([P, width], U32, name=f"{name}_codes", align_bytes=64, offset=codes_at)
-            if scales_at is None:
-                scales = keep.tile([P, width], U8, name=f"{name}_scales", align_bytes=64)
-            else:
-                scales = shared.tile([P, width], U8, name=f"{name}_scales", align_bytes=64, offset=scales_at)
-            return codes, scales
+            return place(f"{name}_codes", width, U32, codes_at), place(f"{name}_scales", width, U8, scales_at)
 
         def quantize(target, quads):
             nc.vector.quantize_mx(
@@ -96,8 +104,21 @@ def tile_attend_x_mla_cap_srt_kernel(tc, qT, cT, ts, ch, offs, out):
             for u in range(2):
                 nc.tensor.transpose(turned[:, u, :], words[:, u, :], ident[:])
 
-        def halves(picked):
-            return picked.rearrange("p u (h s) e -> p h u (s e)", h=2)
+        def halves(dealt):
+            return dealt.rearrange("p u (h s) e -> p h u (s e)", h=2)
+
+        def copy_values(quads, turned):
+            nc.scalar.copy(
+                quads[:].bitcast(F32).rearrange("s h (t p) u -> s h t p u", t=2),
+                turned[:].rearrange("s t u (h p) -> s h t p u", h=2),
+            )
+
+        k_quads = [keep.tile([P, HALF, PACK], BF16, name=f"k_quads{h}", align_bytes=64) for h in range(2)]
+        k_places = [k_quads[h][:].rearrange("p (u c) t -> p u c t", u=2) for h in range(2)]
+        first = keep.tile([P, 2, P, 2], BF16, name="first", align_bytes=64)
+        gather(0, first[:])
+        for h in range(2):
+            nc.vector.tensor_copy(k_places[h][:, :, :, 0], halves(first[:])[:, h])
 
         ts_picked = keep.tile([P, PACK, P], F32, name="ts_picked")
         nc.vector.tensor_copy(ts_picked[:].rearrange("p c s -> p (c s)"), ts_table[:].indirect(offsets[:]))
@@ -112,15 +133,9 @@ def tile_attend_x_mla_cap_srt_kernel(tc, qT, cT, ts, ch, offs, out):
         ts_dealt = keep.tile([P, 2, P, 2], F32, name="ts_dealt")
         nc.scalar.copy(ts_dealt[:], ts_spread[:].rearrange("q c (s u e) -> q u (c s) e", u=2, e=2))
 
-        k_quads = [keep.tile([P, HALF, PACK], BF16, name=f"k_quads{h}", align_bytes=64) for h in range(2)]
-        k_places = [k_quads[h][:].rearrange("p (u c) t -> p u c t", u=2) for h in range(2)]
-        first = keep.tile([P, 2, P, 2], BF16, name="first", align_bytes=64)
-        gather(0, first[:])
-        for h in range(2):
-            nc.vector.tensor_copy(k_places[h][:, :, :, 0], halves(first[:])[:, h])
         turned_early = psum.tile([P, 2, 2, P], F32, name="turned_early", tag="bank_a1")
         turn(first[:], turned_early[:, 0])
-        pair = shared.tile([P, 2, 2, P, 2], BF16, name="pair", align_bytes=64, offset=0)
+        pair = shared.tile([P, 2, 2, P, 2], BF16, name="pair", align_bytes=64, offset=PAIR_AT)
         gather(1, pair[:, 0])
         turn(pair[:, 0], turned_early[:, 1])
         gather(3, pair[:, 1])
@@ -134,7 +149,7 @@ def tile_attend_x_mla_cap_srt_kernel(tc, qT, cT, ts, ch, offs, out):
         for h in range(2):
             nc.vector.tensor_copy(
                 last[:].rearrange("p u s e -> p s u e")[:, h * P // 2 : (h + 1) * P // 2],
-                planes[2][:].indirect(offsets[:, h * HALF // 16 : (h + 1) * HALF // 16]),
+                planes[2][:].indirect(offsets[:, h * HALF // LIST_ROWS : (h + 1) * HALF // LIST_ROWS]),
             )
         for h in range(2):
             nc.vector.tensor_copy(k_places[h][:, :, :, 1], halves(last[:])[:, h])
@@ -142,27 +157,21 @@ def tile_attend_x_mla_cap_srt_kernel(tc, qT, cT, ts, ch, offs, out):
 
         q_quads = []
         for b in range(BLOCKS):
-            q_quads.append(shared.tile([P, P, PACK], BF16, name=f"q_quads{b}", align_bytes=64, offset=1024 * b))
+            q_quads.append(shared.tile([P, P, PACK], BF16, name=f"q_quads{b}", align_bytes=64, offset=PAIR_AT + KIB * b))
             nc.scalar.copy(
                 q_quads[b][:].rearrange("p q (w e) -> p q w e", w=2), q_raw[b][:].rearrange("p (e w) q -> p q w e", w=2)
             )
-        v_early = shared.tile([P, 2, P, PACK], BF16, name="v_early", align_bytes=64, offset=46464)
-        nc.scalar.copy(
-            v_early[:].bitcast(F32).rearrange("s h (t p) u -> s h t p u", t=2),
-            turned_early[:].rearrange("s t u (h p) -> s h t p u", h=2),
-        )
-        v_late = shared.tile([P, 2, P, PACK], BF16, name="v_late", align_bytes=64, offset=43264)
-        nc.scalar.copy(
-            v_late[:].bitcast(F32).rearrange("s h (t p) u -> s h t p u", t=2),
-            turned_late[:].rearrange("s t u (h p) -> s h t p u", h=2),
-        )
-        last_plane = 8192 * 3
-        keys = [operand("k0", HALF, last_plane), operand("k1", HALF, 40960)]
-        queries = [operand(f"q{b}", P, last_plane + 1024 * (b + 1)) for b in range(BLOCKS)]
+        v_early = shared.tile([P, 2, P, PACK], BF16, name="v_early", align_bytes=64, offset=V_EARLY_AT)
+        copy_values(v_early, turned_early)
+        v_late = shared.tile([P, 2, P, PACK], BF16, name="v_late", align_bytes=64, offset=V_LATE_AT)
+        copy_values(v_late, turned_late)
+
+        keys = [operand("k0", HALF, LAST_PLANE_AT), operand("k1", HALF, Q_RAW_AT[0])]
+        queries = [operand(f"q{b}", P, LAST_PLANE_AT + KIB * (b + 1)) for b in range(BLOCKS)]
         for n in range(2):
             quantize(keys[n], k_quads[n][:])
             quantize(queries[n], q_quads[n][:])
-        values = [[operand("v00", P, scales_at=45312)], []]
+        values = [[operand("v00", P, scales_at=FIRST_V_SCALES_AT)], []]
         quantize(values[0][0], v_early[:, 0])
         quarters = [(b, h) for b in range(BLOCKS) for h in range(2)]
         scores = {}
@@ -170,15 +179,14 @@ def tile_attend_x_mla_cap_srt_kernel(tc, qT, cT, ts, ch, offs, out):
             scores[b, h] = psum.tile([P, 2, P], F32, name=f"scores{b}{h}", tag=f"bank_b{b}{h}")
             product(scores[b, h][:].rearrange("q u c -> q (u c)"), queries[b], keys[h])
 
-        scaled = {}
         capped = [keep.tile([P, 2, 2, P], F32, name=f"capped{b}") for b in range(BLOCKS)]
         for b, h in quarters:
-            if (b, h) == (0, 0):
-                scaled[b, h] = shared.tile([P, 2, P], F32, name="scaled00", align_bytes=64, offset=45440)
+            if (b, h) == quarters[0]:
+                scaled = shared.tile([P, 2, P], F32, name="scaled00", align_bytes=64, offset=FIRST_SCALED_AT)
             else:
-                scaled[b, h] = keep.tile([P, 2, P], F32, name=f"scaled{b}{h}")
-            nc.vector.tensor_tensor(scaled[b, h][:], scores[b, h][:], halves(ts_dealt[:])[:, h], ALU.mult)
-            nc.scalar.activation(capped[b][:, :, h], scaled[b, h][:], ACT.Tanh, scale=1.0 / CAP)
+                scaled = keep.tile([P, 2, P], F32, name=f"scaled{b}{h}")
+            nc.vector.tensor_tensor(scaled[:], scores[b, h][:], halves(ts_dealt[:])[:, h], ALU.mult)
+            nc.scalar.activation(capped[b][:, :, h], scaled[:], ACT.Tanh, scale=1.0 / CAP)
         minus_c, minus_m = [], []
         for b in range(BLOCKS):
             minus_c.append(keep.tile([P, 2, HALF], F32, name=f"minus_c{b}"))
@@ -193,39 +201,43 @@ def tile_attend_x_mla_cap_srt_kernel(tc, qT, cT, ts, ch, offs, out):
                 accum_out=minus_m[b][:],
             )
         total = keep.tile([P, BLOCKS, 2], F32, name="total")
-        w_quads = []
+        w_quads, w_turned = [], []
         for b in range(BLOCKS):
-            w_turned = psum.tile([P, 2, P], F32, name=f"w_turned{b}", tag=f"bank_a{b}")
+            w_turned.append(psum.tile([P, 2, P], F32, name=f"w_turned{b}", tag=f"bank_a{b}"))
             for u in range(2):
-                prob = shared.tile([P, HALF], F32, name=f"prob{b}{u}", align_bytes=64, offset=2048 + 1024 * (2 * b + u))
+                prob = place(f"prob{b}{u}", HALF, F32, PROB_AT + KIB * (2 * b + u))
                 nc.scalar.activation(
                     prob[:], minus_c[b][:, u], ACT.Exp, bias=minus_m[b][:], scale=-1.0, accum_out=total[:, b, u : u + 1]
                 )
                 w_pairs = keep.tile([P, HALF], BF16, name=f"w_pairs{b}{u}", align_bytes=64)
                 nc.vector.tensor_tensor(w_pairs[:], prob[:], ts_dealt[:, u].rearrange("q s e -> q (s e)"), ALU.mult)
-                nc.tensor.transpose(w_turned[:, u, :], w_pairs[:].bitcast(F32), ident[:])
-            w_quads.append((keep.tile([P, P, PACK], BF16, name=f"w_quads{b}", align_bytes=64), w_turned))
-        for quads, w_turned in w_quads:
-            nc.scalar.copy(quads[:].bitcast(F32), w_turned[:].rearrange("s u q -> s q u"))
-        last_prob = 2048 + 1024 * 3
-        values[0].append(operand("v01", P, scales_at=last_prob))
+                nc.tensor.transpose(w_turned[b][:, u, :], w_pairs[:].bitcast(F32), ident[:])
+            w_quads.append(keep.tile([P, P, PACK], BF16, name=f"w_quads{b}", align_bytes=64))
+        for b in range(BLOCKS):
+            nc.scalar.copy(w_quads[b][:].bitcast(F32), w_turned[b][:].rearrange("s u q -> s q u"))
+
+        values[0].append(operand("v01", P, scales_at=LAST_PROB_AT))
         quantize(values[0][1], v_late[:, 0])
-        values[1].extend(operand(f"v1{n}", P, scales_at=last_prob + P * (n + 1)) for n in range(2))
-        weights = [operand("w0", P, scales_at=last_prob + 4 * P), operand("w1", P)]
+        values[1].extend(operand(f"v1{n}", P, scales_at=LAST_PROB_AT + P * (n + 1)) for n in range(2))
+        weights = [operand("w0", P, scales_at=LAST_PROB_AT + 4 * P), operand("w1", P)]
         quantize(values[1][0], v_early[:, 1])
-        quantize(weights[0], w_quads[0][0][:])
+        quantize(weights[0], w_quads[0][:])
         quantize(values[1][1], v_late[:, 1])
         row_sum = keep.tile([P, BLOCKS], F32, name="row_sum")
-        nc.gpsimd.tensor_tensor(row_sum[:], total[:, :, 0], total[:, :, 1], ALU.add)
+        nc.vector.tensor_tensor(row_sum[:], total[:, :, 0], total[:, :, 1], ALU.add)
         inverse = keep.tile([P, BLOCKS], F32, name="inverse")
         nc.vector.reciprocal(inverse[:], row_sum[:])
-        quantize(weights[1], w_quads[1][0][:])
+        quantize(weights[1], w_quads[1][:])
         y = {}
         for b, h in quarters:
             y[b, h] = psum.tile([P, 2, P], F32, name=f"y{b}{h}", tag=f"bank_b{b}{h}")
             for n in range(2):
                 product(y[b, h][:, n, :], weights[b], values[h][n])
-        results = [keep.tile([P, FEATURES], F32, name=f"result{b}", tag=("w_quads1", "result1")[b], align_bytes=64) for b in range(BLOCKS)]
+
+        result_tags = ("w_quads1", "result1")
+        results = [
+            keep.tile([P, FEATURES], F32, name=f"result{b}", tag=result_tags[b], align_bytes=64) for b in range(BLOCKS)
+        ]
         for b, h in quarters:
             columns = slice(h * HALF, (h + 1) * HALF)
             nc.vector.scalar_tensor_tensor(

@@ -23,17 +23,16 @@ HALF = SLOTS // 2
 LIST_ROWS = 16
 CAP = 2.0
 
+
 KIB = 1024
-PAIR_AT = 0
-PROB_AT = 2 * KIB
-LAST_PROB_AT = PROB_AT + 3 * KIB
+LAST_CAPPED_AT = 0
+PAIR_AT = 48 * KIB
+RUN = TOKENS // P
 PLANES_AT = 8 * KIB
-LAST_PLANE_AT = PLANES_AT + 2 * 8 * KIB
+LAST_PLANE_AT = PLANES_AT + 3 * 8 * KIB
 Q_RAW_AT = (40 * KIB, 44 * KIB)
 V_LATE_AT = Q_RAW_AT[1] + 256 - 2 * KIB
-FIRST_V_SCALES_AT = V_LATE_AT + 2 * KIB
-FIRST_SCALED_AT = FIRST_V_SCALES_AT + P
-V_EARLY_AT = FIRST_SCALED_AT + KIB
+FIRST_SCALED_AT = V_LATE_AT + 2 * KIB
 
 FLOPS = 2 * 2 * QUERIES * SLOTS * FEATURES
 
@@ -45,8 +44,8 @@ def tile_attend_x_mla_cap_srt_kernel(tc, qT, cT, ts, ch, offs, out):
         shared = ctx.enter_context(tc.tile_pool(name="shared", bufs=1))
         psum = ctx.enter_context(tc.psum_pool(name="psum", bufs=1))
 
-        ts_table = keep.tile([P, TOKENS], F32, name="ts_table", align_bytes=64)
-        nc.scalar.dma_start(ts_table[P - 1 : P, :], ts[0:1, :])
+        ts_runs = keep.tile([P, RUN], F32, name="ts_runs")
+        nc.sync.dma_start(ts_runs[:], ts[0].rearrange("(p j) -> p j", j=RUN))
         offsets = keep.tile([P, SLOTS // LIST_ROWS], U16, name="offsets")
         plane_rows = cT.rearrange("(p j) w -> j p w", j=PACK)
         planes = [
@@ -55,7 +54,7 @@ def tile_attend_x_mla_cap_srt_kernel(tc, qT, cT, ts, ch, offs, out):
         ]
         nc.sync.dma_start(planes[0][:], plane_rows[0])
         nc.sync.dma_start(offsets[:], offs)
-        for j in (1, 3, 2):
+        for j in (1, 2, 3):
             nc.sync.dma_start(planes[j][:], plane_rows[j])
         q_rows = qT[0].rearrange("(p j) q -> p j q", j=PACK)
         q_raw = []
@@ -65,7 +64,6 @@ def tile_attend_x_mla_cap_srt_kernel(tc, qT, cT, ts, ch, offs, out):
         channel = keep.tile([P, FEATURES], F32, name="channel")
         nc.sync.dma_start(channel[:], ch)
 
-        nc.vector.memset(ts_table[: P - 1, :], 0.0)
         ident = keep.tile([P, P], F32, name="ident")
         make_identity(nc, ident[:])
         warm = keep.tile([P, 1], F32, name="warm")
@@ -80,9 +78,11 @@ def tile_attend_x_mla_cap_srt_kernel(tc, qT, cT, ts, ch, offs, out):
         def operand(name, width, codes_at=None, scales_at=None):
             return place(f"{name}_codes", width, U32, codes_at), place(f"{name}_scales", width, U8, scales_at)
 
-        def quantize(target, quads):
+        def quantize(target, quads, columns=slice(None)):
             nc.vector.quantize_mx(
-                out=target[0][:].bitcast(FP8X4), scales=target[1][:], in_=quads.rearrange("p n j -> p (n j)")
+                out=target[0][:, columns].bitcast(FP8X4),
+                scales=target[1][:, columns],
+                in_=quads.rearrange("p n j -> p (n j)"),
             )
 
         def product(result, stationary, moving):
@@ -99,140 +99,166 @@ def tile_attend_x_mla_cap_srt_kernel(tc, qT, cT, ts, ch, offs, out):
         def gather(j, picked):
             nc.vector.tensor_copy(picked.rearrange("p u s e -> p s u e"), planes[j][:].indirect(offsets[:]))
 
+        def gather_halves(j, picked):
+            for h in range(2):
+                nc.vector.tensor_copy(
+                    picked.rearrange("p u s e -> p s u e")[:, h * P // 2 : (h + 1) * P // 2],
+                    planes[j][:].indirect(offsets[:, h * HALF // LIST_ROWS : (h + 1) * HALF // LIST_ROWS]),
+                )
+
         def turn(picked, turned):
             words = picked.rearrange("p u s e -> p u (s e)").bitcast(F32)
             for u in range(2):
                 nc.tensor.transpose(turned[:, u, :], words[:, u, :], ident[:])
 
         def halves(dealt):
-            return dealt.rearrange("p u (h s) e -> p h u (s e)", h=2)
+            return dealt.rearrange("p u (h s) e -> p h s u e", h=2)
 
         def copy_values(quads, turned):
+            nc.scalar.copy(quads, turned.rearrange("s t u (h p) -> s h t p u", h=2))
+
+        def value_words(name, at):
+            tile = place(name, 2 * P * PACK, BF16, at)
+            quads = tile[:].rearrange("s (h n j) -> s h n j", h=2, j=PACK)
+            return quads, tile[:].bitcast(F32).rearrange("s (h t p u) -> s h t p u", h=2, t=2, u=2)
+
+        quarters = [(b, h) for b in range(BLOCKS) for h in range(2)]
+        ts_table = keep.tile([P, TOKENS], F32, name="ts_table", align_bytes=64)
+        for n, (b, h) in enumerate(quarters):
+            spread = psum.tile([P, PACK, P], F32, name=f"spread{n}", tag=f"bank_b{b}{h}")
+            for j in range(PACK):
+                column = ts_runs[:, PACK * n + j : PACK * n + j + 1]
+                nc.tensor.transpose(spread[:, j, :], column.to_broadcast([P, P]), ident[:])
             nc.scalar.copy(
-                quads[:].bitcast(F32).rearrange("s h (t p) u -> s h t p u", t=2),
-                turned[:].rearrange("s t u (h p) -> s h t p u", h=2),
+                ts_table[:].rearrange("q (p j) -> q p j", j=RUN)[:, :, PACK * n : PACK * (n + 1)],
+                spread[:].rearrange("q j p -> q p j"),
             )
+        ts_rows = keep.tile([P, SLOTS], F32, name="ts_rows")
+        nc.scalar.activation(ts_rows[:], ts_table[:].indirect(offsets[:]), ACT.Copy)
 
         k_quads = [keep.tile([P, HALF, PACK], BF16, name=f"k_quads{h}", align_bytes=64) for h in range(2)]
-        k_places = [k_quads[h][:].rearrange("p (u c) t -> p u c t", u=2) for h in range(2)]
-        first = keep.tile([P, 2, P, 2], BF16, name="first", align_bytes=64)
-        gather(0, first[:])
-        for h in range(2):
-            nc.vector.tensor_copy(k_places[h][:, :, :, 0], halves(first[:])[:, h])
-
-        ts_picked = keep.tile([P, PACK, P], F32, name="ts_picked")
-        nc.vector.tensor_copy(ts_picked[:].rearrange("p c s -> p (c s)"), ts_table[:].indirect(offsets[:]))
-        ts_turned = psum.tile([P, PACK, P], F32, name="ts_turned", tag="bank_a0")
-        for c in range(PACK):
-            nc.tensor.transpose(ts_turned[:, c, :], ts_picked[:, c, :], ident[:])
-        ts_column = keep.tile([P, PACK], F32, name="ts_column")
-        nc.scalar.copy(ts_column[:], ts_turned[:, :, P - 1])
-        ts_spread = psum.tile([P, PACK, P], F32, name="ts_spread", tag="bank_a1")
-        for c in range(PACK):
-            nc.tensor.transpose(ts_spread[:, c, :], ts_column[:, c : c + 1].to_broadcast([P, P]), ident[:])
-        ts_dealt = keep.tile([P, 2, P, 2], F32, name="ts_dealt")
-        nc.scalar.copy(ts_dealt[:], ts_spread[:].rearrange("q c (s u e) -> q u (c s) e", u=2, e=2))
-
-        turned_early = psum.tile([P, 2, 2, P], F32, name="turned_early", tag="bank_a1")
-        turn(first[:], turned_early[:, 0])
+        k_places = [k_quads[h][:].rearrange("p (s u e) t -> p s u e t", u=2, e=2) for h in range(2)]
         pair = shared.tile([P, 2, 2, P, 2], BF16, name="pair", align_bytes=64, offset=PAIR_AT)
-        gather(1, pair[:, 0])
-        turn(pair[:, 0], turned_early[:, 1])
-        gather(3, pair[:, 1])
-        turned_late = psum.tile([P, 2, 2, P], F32, name="turned_late", tag="bank_a3")
-        turn(pair[:, 1], turned_late[:, 1])
-        pair_halves = pair[:].rearrange("p t u (h s) e -> p h u (s e) t", h=2)
-        nc.vector.tensor_copy(k_places[0][:, 0, :, 2:4], pair_halves[:, 0, 0])
-        nc.scalar.copy(k_places[0][:, 1, :, 2:4], pair_halves[:, 0, 1])
-        nc.scalar.copy(k_places[1][:, :, :, 2:4], pair_halves[:, 1])
-        last = keep.tile([P, 2, P, 2], BF16, name="last", align_bytes=64)
+        gather(0, pair[:, 0])
+
+        v_early, v_early_words = value_words("v_early", None)
+        gather_halves(1, pair[:, 1])
+        turned_early = psum.tile([P, 2, 2, P], F32, name="turned_early", tag="bank_b11")
+        for t in range(2):
+            turn(pair[:, t], turned_early[:, t])
+        copy_values(v_early_words, turned_early[:])
+        ts_turned = psum.tile([P, PACK, P], F32, name="ts_turned", tag="bank_a2")
+        for t in range(PACK):
+            nc.tensor.transpose(ts_turned[:, t, :], ts_rows[:].rearrange("q (s t) -> q t s", t=PACK)[:, t], ident[:])
+        ts_column = keep.tile([P, PACK], F32, name="ts_column")
+        nc.scalar.copy(ts_column[:], ts_turned[:, :, 0])
+        pair_halves = pair[:].rearrange("p t u (h s) e -> p h s u e t", h=2)
         for h in range(2):
-            nc.vector.tensor_copy(
-                last[:].rearrange("p u s e -> p s u e")[:, h * P // 2 : (h + 1) * P // 2],
-                planes[2][:].indirect(offsets[:, h * HALF // LIST_ROWS : (h + 1) * HALF // LIST_ROWS]),
-            )
+            nc.vector.tensor_copy(k_places[h][:, :, :, :, 0:2], pair_halves[:, h])
+        third = keep.tile([P, 2, P, 2], BF16, name="third", align_bytes=64)
+        gather_halves(2, third[:])
         for h in range(2):
-            nc.vector.tensor_copy(k_places[h][:, :, :, 1], halves(last[:])[:, h])
-        turn(last[:], turned_late[:, 0])
+            nc.vector.tensor_copy(k_places[h][:, :, :, :, 2], halves(third[:])[:, h])
+        turned_late = psum.tile([P, 2, 2, P], F32, name="turned_late", tag="bank_a2")
+        turn(third[:], turned_late[:, 0])
+        last = shared.tile([P, SLOTS], BF16, name="last", align_bytes=64, offset=PAIR_AT)
+        cut = HALF // LIST_ROWS
+        nc.vector.tensor_copy(last[:, :HALF], planes[3][:].indirect(offsets[:, :cut]))
+        nc.scalar.activation(last[:, HALF:], planes[3][:].indirect(offsets[:, cut:]), ACT.Copy)
+        last_halves = last[:].rearrange("p (h s u e) -> p h s u e", h=2, u=2, e=2)
+        for h in range(2):
+            nc.vector.tensor_copy(k_places[h][:, :, :, :, 3], last_halves[:, h])
+        last_words = last[:].bitcast(F32).rearrange("p (s u) -> p u s", u=2)
+        for u in range(2):
+            nc.tensor.transpose(turned_late[:, 1, u, :], last_words[:, u, :], ident[:])
 
         q_quads = []
         for b in range(BLOCKS):
-            q_quads.append(shared.tile([P, P, PACK], BF16, name=f"q_quads{b}", align_bytes=64, offset=PAIR_AT + KIB * b))
-            nc.scalar.copy(
-                q_quads[b][:].rearrange("p q (w e) -> p q w e", w=2), q_raw[b][:].rearrange("p (e w) q -> p q w e", w=2)
+            q_quads.append(
+                shared.tile([P, P, PACK], BF16, name=f"q_quads{b}", align_bytes=64, offset=(PAIR_AT + KIB, LAST_PLANE_AT)[b])
             )
-        v_early = shared.tile([P, 2, P, PACK], BF16, name="v_early", align_bytes=64, offset=V_EARLY_AT)
-        copy_values(v_early, turned_early)
-        v_late = shared.tile([P, 2, P, PACK], BF16, name="v_late", align_bytes=64, offset=V_LATE_AT)
-        copy_values(v_late, turned_late)
+            nc.scalar.copy(
+                q_quads[b][:].rearrange("p (c i) j -> p c j i", i=PACK),
+                q_raw[b][:].rearrange("p j (c i) -> p c j i", i=PACK),
+            )
+        v_late, v_late_words = value_words("v_late", V_LATE_AT)
+        copy_values(v_late_words, turned_late[:])
 
-        keys = [operand("k0", HALF, LAST_PLANE_AT), operand("k1", HALF, Q_RAW_AT[0])]
-        queries = [operand(f"q{b}", P, LAST_PLANE_AT + KIB * (b + 1)) for b in range(BLOCKS)]
+        keys = [operand("k0", HALF, LAST_PLANE_AT + 2 * KIB), operand("k1", HALF, Q_RAW_AT[0])]
+        queries = [operand(f"q{b}", P, LAST_PLANE_AT + KIB * (b + 3)) for b in range(BLOCKS)]
         for n in range(2):
             quantize(keys[n], k_quads[n][:])
             quantize(queries[n], q_quads[n][:])
-        values = [[operand("v00", P, scales_at=FIRST_V_SCALES_AT)], []]
-        quantize(values[0][0], v_early[:, 0])
-        quarters = [(b, h) for b in range(BLOCKS) for h in range(2)]
         scores = {}
         for b, h in quarters:
-            scores[b, h] = psum.tile([P, 2, P], F32, name=f"scores{b}{h}", tag=f"bank_b{b}{h}")
-            product(scores[b, h][:].rearrange("q u c -> q (u c)"), queries[b], keys[h])
+            scores[b, h] = psum.tile([P, HALF], F32, name=f"scores{b}{h}", tag=f"bank_b{b}{h}")
+            product(scores[b, h][:], queries[b], keys[h])
 
-        capped = [keep.tile([P, 2, 2, P], F32, name=f"capped{b}") for b in range(BLOCKS)]
+        capped = [
+            keep.tile([P, PACK, P], F32, name="capped0"),
+            shared.tile([P, PACK, P], F32, name="capped1", align_bytes=64, offset=LAST_CAPPED_AT),
+        ]
         for b, h in quarters:
             if (b, h) == quarters[0]:
-                scaled = shared.tile([P, 2, P], F32, name="scaled00", align_bytes=64, offset=FIRST_SCALED_AT)
+                scaled = shared.tile([P, HALF], F32, name="scaled00", align_bytes=64, offset=FIRST_SCALED_AT)
             else:
-                scaled = keep.tile([P, 2, P], F32, name=f"scaled{b}{h}")
-            nc.vector.tensor_tensor(scaled[:], scores[b, h][:], halves(ts_dealt[:])[:, h], ALU.mult)
-            nc.scalar.activation(capped[b][:, :, h], scaled[:], ACT.Tanh, scale=1.0 / CAP)
+                scaled = keep.tile([P, HALF], F32, name=f"scaled{b}{h}")
+            part = slice(h * P // 2, (h + 1) * P // 2)
+            nc.vector.tensor_tensor(scaled[:], scores[b, h][:], ts_rows[:, h * HALF : (h + 1) * HALF], ALU.mult)
+            nc.scalar.activation(
+                capped[b][:].rearrange("q t s -> q s t")[:, part],
+                scaled[:].rearrange("q (s t) -> q s t", t=PACK),
+                ACT.Tanh,
+                scale=1.0 / CAP,
+            )
         minus_c, minus_m = [], []
         for b in range(BLOCKS):
-            minus_c.append(keep.tile([P, 2, HALF], F32, name=f"minus_c{b}"))
+            minus_c.append(keep.tile([P, PACK, P], F32, name=f"minus_c{b}"))
             minus_m.append(keep.tile([P, 1], F32, name=f"minus_m{b}"))
             nc.vector.tensor_scalar(
-                minus_c[b][:],
-                capped[b][:].rearrange("q u h c -> q u (h c)"),
-                -CAP,
-                None,
-                ALU.mult,
-                ALU.min,
-                accum_out=minus_m[b][:],
+                minus_c[b][:], capped[b][:], -CAP, None, ALU.mult, ALU.min, accum_out=minus_m[b][:]
             )
+        values = [operand(f"v{h}", HALF, scales_at=LAST_CAPPED_AT + HALF * h) for h in range(2)]
+        for h in range(2):
+            for n, quads in enumerate((v_early, v_late)):
+                quantize(values[h], quads[:, h], slice(n * P, (n + 1) * P))
         total = keep.tile([P, BLOCKS, 2], F32, name="total")
-        w_quads, w_turned = [], []
+        p_turned = []
         for b in range(BLOCKS):
-            w_turned.append(psum.tile([P, 2, P], F32, name=f"w_turned{b}", tag=f"bank_a{b}"))
+            p_turned.append(psum.tile([P, PACK, P], F32, name=f"p_turned{b}", tag=f"bank_a{b}"))
             for u in range(2):
-                prob = place(f"prob{b}{u}", HALF, F32, PROB_AT + KIB * (2 * b + u))
+                prob = keep.tile([P, 2, P], F32, name=f"prob{b}{u}")
                 nc.scalar.activation(
-                    prob[:], minus_c[b][:, u], ACT.Exp, bias=minus_m[b][:], scale=-1.0, accum_out=total[:, b, u : u + 1]
+                    prob[:],
+                    minus_c[b][:, 2 * u : 2 * u + 2],
+                    ACT.Exp,
+                    bias=minus_m[b][:],
+                    scale=-1.0,
+                    accum_out=total[:, b, u : u + 1],
                 )
-                w_pairs = keep.tile([P, HALF], BF16, name=f"w_pairs{b}{u}", align_bytes=64)
-                nc.vector.tensor_tensor(w_pairs[:], prob[:], ts_dealt[:, u].rearrange("q s e -> q (s e)"), ALU.mult)
-                nc.tensor.transpose(w_turned[b][:, u, :], w_pairs[:].bitcast(F32), ident[:])
-            w_quads.append(keep.tile([P, P, PACK], BF16, name=f"w_quads{b}", align_bytes=64))
-        for b in range(BLOCKS):
-            nc.scalar.copy(w_quads[b][:].bitcast(F32), w_turned[b][:].rearrange("s u q -> s q u"))
-
-        values[0].append(operand("v01", P, scales_at=LAST_PROB_AT))
-        quantize(values[0][1], v_late[:, 0])
-        values[1].extend(operand(f"v1{n}", P, scales_at=LAST_PROB_AT + P * (n + 1)) for n in range(2))
-        weights = [operand("w0", P, scales_at=LAST_PROB_AT + 4 * P), operand("w1", P)]
-        quantize(values[1][0], v_early[:, 1])
-        quantize(weights[0], w_quads[0][:])
-        quantize(values[1][1], v_late[:, 1])
+                for e in range(2):
+                    nc.tensor.transpose(p_turned[b][:, 2 * u + e, :], prob[:, e, :], ident[:])
         row_sum = keep.tile([P, BLOCKS], F32, name="row_sum")
-        nc.vector.tensor_tensor(row_sum[:], total[:, :, 0], total[:, :, 1], ALU.add)
         inverse = keep.tile([P, BLOCKS], F32, name="inverse")
-        nc.vector.reciprocal(inverse[:], row_sum[:])
-        quantize(weights[1], w_quads[1][:])
+        ts_places = ts_column[:].unsqueeze(1).to_broadcast([P, P // 2, PACK])
+        weights = []
+        for b in range(BLOCKS):
+            w_quads = keep.tile([P, P, PACK], BF16, name=f"w_quads{b}", align_bytes=64)
+            weights.append(operand(f"w{b}", P))
+            parts = [slice(g * P // 2, (g + 1) * P // 2) for g in range(2)]
+            for part in parts:
+                nc.vector.tensor_tensor(
+                    w_quads[:, part], p_turned[b][:].rearrange("s t q -> s q t")[:, part], ts_places, ALU.mult
+                )
+            for part in parts:
+                quantize(weights[b], w_quads[:, part], part)
+            if b == 0:
+                nc.vector.tensor_tensor(row_sum[:], total[:, :, 0], total[:, :, 1], ALU.add)
+                nc.vector.reciprocal(inverse[:], row_sum[:])
         y = {}
         for b, h in quarters:
-            y[b, h] = psum.tile([P, 2, P], F32, name=f"y{b}{h}", tag=f"bank_b{b}{h}")
-            for n in range(2):
-                product(y[b, h][:, n, :], weights[b], values[h][n])
+            y[b, h] = psum.tile([P, PACK, P // 2], F32, name=f"y{b}{h}", tag=f"bank_b{b}{h}")
+            product(y[b, h][:].rearrange("q t p -> q (t p)"), weights[b], values[h])
 
         result_tags = ("w_quads1", "result1")
         results = [
@@ -242,7 +268,7 @@ def tile_attend_x_mla_cap_srt_kernel(tc, qT, cT, ts, ch, offs, out):
             columns = slice(h * HALF, (h + 1) * HALF)
             nc.vector.scalar_tensor_tensor(
                 results[b][:, columns].rearrange("q (p t) -> q p t", t=PACK),
-                y[b, h][:].rearrange("q n (t p) -> q p (n t)", t=2),
+                y[b, h][:].rearrange("q t p -> q p t"),
                 inverse[:, b : b + 1],
                 channel[:, columns].rearrange("q (p t) -> q p t", t=PACK),
                 ALU.mult,

@@ -26,6 +26,8 @@ CAP = 2.0
 
 KIB = 1024
 LAST_CAPPED_AT = 0
+LAST_MINUS_C_AT = 4 * KIB
+TS_COLUMN_AT = 6 * KIB
 PAIR_AT = 48 * KIB
 RUN = TOKENS // P
 PLANES_AT = 8 * KIB
@@ -45,7 +47,6 @@ def tile_attend_x_mla_cap_srt_kernel(tc, qT, cT, ts, ch, offs, out):
         psum = ctx.enter_context(tc.psum_pool(name="psum", bufs=1))
 
         ts_runs = keep.tile([P, RUN], F32, name="ts_runs")
-        nc.sync.dma_start(ts_runs[:], ts[0].rearrange("(p j) -> p j", j=RUN))
         offsets = keep.tile([P, SLOTS // LIST_ROWS], U16, name="offsets")
         plane_rows = cT.rearrange("(p j) w -> j p w", j=PACK)
         planes = [
@@ -53,6 +54,7 @@ def tile_attend_x_mla_cap_srt_kernel(tc, qT, cT, ts, ch, offs, out):
             for j in range(PACK)
         ]
         nc.sync.dma_start(planes[0][:], plane_rows[0])
+        nc.sync.dma_start(ts_runs[:], ts[0].rearrange("(p j) -> p j", j=RUN))
         nc.sync.dma_start(offsets[:], offs)
         for j in (1, 2, 3):
             nc.sync.dma_start(planes[j][:], plane_rows[j])
@@ -150,7 +152,7 @@ def tile_attend_x_mla_cap_srt_kernel(tc, qT, cT, ts, ch, offs, out):
         ts_turned = psum.tile([P, PACK, P], F32, name="ts_turned", tag="bank_a2")
         for t in range(PACK):
             nc.tensor.transpose(ts_turned[:, t, :], ts_rows[:].rearrange("q (s t) -> q t s", t=PACK)[:, t], ident[:])
-        ts_column = keep.tile([P, PACK], F32, name="ts_column")
+        ts_column = place("ts_column", PACK, F32, TS_COLUMN_AT)
         nc.scalar.copy(ts_column[:], ts_turned[:, :, 0])
         pair_halves = pair[:].rearrange("p t u (h s) e -> p h s u e t", h=2)
         for h in range(2):
@@ -213,57 +215,66 @@ def tile_attend_x_mla_cap_srt_kernel(tc, qT, cT, ts, ch, offs, out):
             )
         minus_c, minus_m = [], []
         for b in range(BLOCKS):
-            minus_c.append(keep.tile([P, PACK, P], F32, name=f"minus_c{b}"))
+            at = (None, LAST_MINUS_C_AT)[b]
+            minus_c.append(place(f"minus_c{b}", SLOTS, F32, at)[:].rearrange("q (t s) -> q t s", t=PACK))
             minus_m.append(keep.tile([P, 1], F32, name=f"minus_m{b}"))
             nc.vector.tensor_scalar(
-                minus_c[b][:], capped[b][:], -CAP, None, ALU.mult, ALU.min, accum_out=minus_m[b][:]
+                minus_c[b], capped[b][:], -CAP, None, ALU.mult, ALU.min, accum_out=minus_m[b][:]
             )
         values = [operand(f"v{h}", HALF, scales_at=LAST_CAPPED_AT + HALF * h) for h in range(2)]
         for h in range(2):
             for n, quads in enumerate((v_early, v_late)):
                 quantize(values[h], quads[:, h], slice(n * P, (n + 1) * P))
-        total = keep.tile([P, BLOCKS, 2], F32, name="total")
+        parts = ((0, 2), (2, 3), (3, 4))
+        total = keep.tile([P, BLOCKS, len(parts)], F32, name="total")
         p_turned = []
         for b in range(BLOCKS):
             p_turned.append(psum.tile([P, PACK, P], F32, name=f"p_turned{b}", tag=f"bank_a{b}"))
-            for u in range(2):
-                prob = keep.tile([P, 2, P], F32, name=f"prob{b}{u}")
+            for n, (lo, hi) in enumerate(parts):
+                prob = keep.tile([P, hi - lo, P], F32, name=f"prob{b}{n}")
                 nc.scalar.activation(
                     prob[:],
-                    minus_c[b][:, 2 * u : 2 * u + 2],
+                    minus_c[b][:, lo:hi],
                     ACT.Exp,
                     bias=minus_m[b][:],
                     scale=-1.0,
-                    accum_out=total[:, b, u : u + 1],
+                    accum_out=total[:, b, n : n + 1],
                 )
-                for e in range(2):
-                    nc.tensor.transpose(p_turned[b][:, 2 * u + e, :], prob[:, e, :], ident[:])
+                for t in range(lo, hi):
+                    nc.tensor.transpose(p_turned[b][:, t, :], prob[:, t - lo, :], ident[:])
+        part_sum = place("part_sum", BLOCKS, F32, LAST_MINUS_C_AT)
         row_sum = keep.tile([P, BLOCKS], F32, name="row_sum")
-        inverse = keep.tile([P, BLOCKS], F32, name="inverse")
-        ts_places = ts_column[:].unsqueeze(1).to_broadcast([P, P // 2, PACK])
-        weights = []
         for b in range(BLOCKS):
-            w_quads = keep.tile([P, P, PACK], BF16, name=f"w_quads{b}", align_bytes=64)
-            weights.append(operand(f"w{b}", P))
-            parts = [slice(g * P // 2, (g + 1) * P // 2) for g in range(2)]
-            for part in parts:
-                nc.vector.tensor_tensor(
-                    w_quads[:, part], p_turned[b][:].rearrange("s t q -> s q t")[:, part], ts_places, ALU.mult
-                )
-            for part in parts:
-                quantize(weights[b], w_quads[:, part], part)
-            if b == 0:
-                nc.vector.tensor_tensor(row_sum[:], total[:, :, 0], total[:, :, 1], ALU.add)
-                nc.vector.reciprocal(inverse[:], row_sum[:])
+            nc.scalar.activation(part_sum[:, b : b + 1], total[:, b, 0:1], ACT.Identity, bias=total[:, b, 1:2])
+        for b in range(BLOCKS):
+            nc.scalar.activation(row_sum[:, b : b + 1], part_sum[:, b : b + 1], ACT.Identity, bias=total[:, b, 2:3])
+        w_quads = [keep.tile([P, P, PACK], BF16, name=f"w_quads{b}", align_bytes=64) for b in range(BLOCKS)]
+        weights = [operand(f"w{b}", P) for b in range(BLOCKS)]
+
+        def weigh(b, lo, hi):
+            nc.vector.tensor_tensor(
+                w_quads[b][:, lo:hi],
+                p_turned[b][:].rearrange("s t q -> s q t")[:, lo:hi],
+                ts_column[:].unsqueeze(1).to_broadcast([P, hi - lo, PACK]),
+                ALU.mult,
+            )
+
+        weigh(0, 0, P // 2)
+        weigh(0, P // 2, P)
+        quantize(weights[0], w_quads[0][:, : P // 2], slice(0, P // 2))
+        weigh(1, 0, P // 2)
+        quantize(weights[0], w_quads[0][:, P // 2 :], slice(P // 2, P))
+        weigh(1, P // 2, P)
+        quantize(weights[1], w_quads[1][:, : P // 2], slice(0, P // 2))
+        inverse = keep.tile([P, BLOCKS], F32, name="inverse")
+        nc.vector.reciprocal(inverse[:], row_sum[:])
+        quantize(weights[1], w_quads[1][:, P // 2 :], slice(P // 2, P))
         y = {}
         for b, h in quarters:
             y[b, h] = psum.tile([P, PACK, P // 2], F32, name=f"y{b}{h}", tag=f"bank_b{b}{h}")
             product(y[b, h][:].rearrange("q t p -> q (t p)"), weights[b], values[h])
 
-        result_tags = ("w_quads1", "result1")
-        results = [
-            keep.tile([P, FEATURES], F32, name=f"result{b}", tag=result_tags[b], align_bytes=64) for b in range(BLOCKS)
-        ]
+        results = [place("result0", FEATURES, F32, TS_COLUMN_AT), place("result1", FEATURES, F32, None)]
         for b, h in quarters:
             columns = slice(h * HALF, (h + 1) * HALF)
             nc.vector.scalar_tensor_tensor(

@@ -27,14 +27,16 @@ CAP = 2.0
 KIB = 1024
 LAST_CAPPED_AT = 0
 LAST_MINUS_C_AT = 4 * KIB
-TS_COLUMN_AT = 6 * KIB
 PAIR_AT = 48 * KIB
 RUN = TOKENS // P
 PLANES_AT = 8 * KIB
 LAST_PLANE_AT = PLANES_AT + 3 * 8 * KIB
-Q_RAW_AT = (40 * KIB, 44 * KIB)
-V_LATE_AT = Q_RAW_AT[1] + 256 - 2 * KIB
+Q_RAW_AT = 42 * KIB
+V_LATE_AT = Q_RAW_AT
 FIRST_SCALED_AT = V_LATE_AT + 2 * KIB
+TS_COLUMN_AT = FIRST_SCALED_AT + KIB
+
+SPREAD_BANKS = ("bank_b00", "bank_b01", "bank_b10", "bank_a2")
 
 FLOPS = 2 * 2 * QUERIES * SLOTS * FEATURES
 
@@ -59,10 +61,8 @@ def tile_attend_x_mla_cap_srt_kernel(tc, qT, cT, ts, ch, offs, out):
         for j in (1, 2, 3):
             nc.sync.dma_start(planes[j][:], plane_rows[j])
         q_rows = qT[0].rearrange("(p j) q -> p j q", j=PACK)
-        q_raw = []
-        for b in range(BLOCKS):
-            q_raw.append(shared.tile([P, PACK, P], F32, name=f"q_raw{b}", align_bytes=64, offset=Q_RAW_AT[b]))
-            nc.sync.dma_start(q_raw[b][:], q_rows[:, :, b * P : (b + 1) * P])
+        q_raw = shared.tile([P, PACK, QUERIES], F32, name="q_raw", align_bytes=64, offset=Q_RAW_AT)
+        nc.sync.dma_start(q_raw[:], q_rows)
         channel = keep.tile([P, FEATURES], F32, name="channel")
         nc.sync.dma_start(channel[:], ch)
 
@@ -126,8 +126,8 @@ def tile_attend_x_mla_cap_srt_kernel(tc, qT, cT, ts, ch, offs, out):
 
         quarters = [(b, h) for b in range(BLOCKS) for h in range(2)]
         ts_table = keep.tile([P, TOKENS], F32, name="ts_table", align_bytes=64)
-        for n, (b, h) in enumerate(quarters):
-            spread = psum.tile([P, PACK, P], F32, name=f"spread{n}", tag=f"bank_b{b}{h}")
+        for n in range(RUN // PACK):
+            spread = psum.tile([P, PACK, P], F32, name=f"spread{n}", tag=SPREAD_BANKS[n])
             for j in range(PACK):
                 column = ts_runs[:, PACK * n + j : PACK * n + j + 1]
                 nc.tensor.transpose(spread[:, j, :], column.to_broadcast([P, P]), ident[:])
@@ -145,15 +145,13 @@ def tile_attend_x_mla_cap_srt_kernel(tc, qT, cT, ts, ch, offs, out):
 
         v_early, v_early_words = value_words("v_early", None)
         gather_halves(1, pair[:, 1])
-        turned_early = psum.tile([P, 2, 2, P], F32, name="turned_early", tag="bank_b11")
+        turned_early = psum.tile([P, 2, 2, P], F32, name="turned_early", tag="bank_a2")
         for t in range(2):
             turn(pair[:, t], turned_early[:, t])
         copy_values(v_early_words, turned_early[:])
-        ts_turned = psum.tile([P, PACK, P], F32, name="ts_turned", tag="bank_a2")
+        ts_turned = psum.tile([P, PACK, P], F32, name="ts_turned", tag="bank_a1")
         for t in range(PACK):
             nc.tensor.transpose(ts_turned[:, t, :], ts_rows[:].rearrange("q (s t) -> q t s", t=PACK)[:, t], ident[:])
-        ts_column = place("ts_column", PACK, F32, TS_COLUMN_AT)
-        nc.scalar.copy(ts_column[:], ts_turned[:, :, 0])
         pair_halves = pair[:].rearrange("p t u (h s) e -> p h s u e t", h=2)
         for h in range(2):
             nc.vector.tensor_copy(k_places[h][:, :, :, :, 0:2], pair_halves[:, h])
@@ -181,16 +179,19 @@ def tile_attend_x_mla_cap_srt_kernel(tc, qT, cT, ts, ch, offs, out):
             )
             nc.scalar.copy(
                 q_quads[b][:].rearrange("p (c i) j -> p c j i", i=PACK),
-                q_raw[b][:].rearrange("p j (c i) -> p c j i", i=PACK),
+                q_raw[:, :, b * P : (b + 1) * P].rearrange("p j (c i) -> p c j i", i=PACK),
             )
+        ts_column = place("ts_column", PACK, F32, TS_COLUMN_AT)
+        nc.scalar.copy(ts_column[:], ts_turned[:, :, 0])
         v_late, v_late_words = value_words("v_late", V_LATE_AT)
         copy_values(v_late_words, turned_late[:])
 
-        keys = [operand("k0", HALF, LAST_PLANE_AT + 2 * KIB), operand("k1", HALF, Q_RAW_AT[0])]
+        keys = [operand(f"k{h}", HALF, LAST_PLANE_AT + KIB * (h + 1)) for h in range(2)]
         queries = [operand(f"q{b}", P, LAST_PLANE_AT + KIB * (b + 3)) for b in range(BLOCKS)]
-        for n in range(2):
-            quantize(keys[n], k_quads[n][:])
-            quantize(queries[n], q_quads[n][:])
+        for h in range(2):
+            quantize(keys[h], k_quads[h][:])
+        for b in range(BLOCKS):
+            quantize(queries[b], q_quads[b][:])
         scores = {}
         for b, h in quarters:
             scores[b, h] = psum.tile([P, HALF], F32, name=f"scores{b}{h}", tag=f"bank_b{b}{h}")

@@ -49,6 +49,7 @@ def tile_attend_x_mla_cap_srt_kernel(tc, qT, cT, ts, ch, offs, out):
         psum = ctx.enter_context(tc.psum_pool(name="psum", bufs=1))
 
         ts_runs = keep.tile([P, RUN], F32, name="ts_runs")
+        nc.scalar.dma_start(ts_runs[:], ts[0].rearrange("(p j) -> p j", j=RUN))
         offsets = keep.tile([P, SLOTS // LIST_ROWS], U16, name="offsets")
         plane_rows = cT.rearrange("(p j) w -> j p w", j=PACK)
         planes = [
@@ -56,7 +57,6 @@ def tile_attend_x_mla_cap_srt_kernel(tc, qT, cT, ts, ch, offs, out):
             for j in range(PACK)
         ]
         nc.sync.dma_start(planes[0][:], plane_rows[0])
-        nc.sync.dma_start(ts_runs[:], ts[0].rearrange("(p j) -> p j", j=RUN))
         nc.sync.dma_start(offsets[:], offs)
         for j in (1, 2, 3):
             nc.sync.dma_start(planes[j][:], plane_rows[j])

@@ -21,20 +21,20 @@ FEATURES = 512
 BLOCKS = QUERIES // P
 HALF = SLOTS // 2
 LIST_ROWS = 16
+RUN = TOKENS // P
 CAP = 2.0
-
+EXP_PARTS = ((0, 2), (2, 3), (3, 4))
 
 KIB = 1024
 LAST_CAPPED_AT = 0
 LAST_MINUS_C_AT = 4 * KIB
-PAIR_AT = 48 * KIB
-RUN = TOKENS // P
 PLANES_AT = 8 * KIB
 LAST_PLANE_AT = PLANES_AT + 3 * 8 * KIB
 Q_RAW_AT = 42 * KIB
 V_LATE_AT = Q_RAW_AT
 FIRST_SCALED_AT = V_LATE_AT + 2 * KIB
 TS_COLUMN_AT = FIRST_SCALED_AT + KIB
+PAIR_AT = 48 * KIB
 
 SPREAD_BANKS = ("bank_b00", "bank_b01", "bank_b10", "bank_a2")
 
@@ -60,9 +60,8 @@ def tile_attend_x_mla_cap_srt_kernel(tc, qT, cT, ts, ch, offs, out):
         nc.sync.dma_start(offsets[:], offs)
         for j in (1, 2, 3):
             nc.sync.dma_start(planes[j][:], plane_rows[j])
-        q_rows = qT[0].rearrange("(p j) q -> p j q", j=PACK)
         q_raw = shared.tile([P, PACK, QUERIES], F32, name="q_raw", align_bytes=64, offset=Q_RAW_AT)
-        nc.sync.dma_start(q_raw[:], q_rows)
+        nc.sync.dma_start(q_raw[:], qT[0].rearrange("(p j) q -> p j q", j=PACK))
         channel = keep.tile([P, FEATURES], F32, name="channel")
         nc.sync.dma_start(channel[:], ch)
 
@@ -113,16 +112,13 @@ def tile_attend_x_mla_cap_srt_kernel(tc, qT, cT, ts, ch, offs, out):
             for u in range(2):
                 nc.tensor.transpose(turned[:, u, :], words[:, u, :], ident[:])
 
-        def halves(dealt):
-            return dealt.rearrange("p u (h s) e -> p h s u e", h=2)
-
-        def copy_values(quads, turned):
-            nc.scalar.copy(quads, turned.rearrange("s t u (h p) -> s h t p u", h=2))
-
-        def value_words(name, at):
+        def value_tile(name, at):
             tile = place(name, 2 * P * PACK, BF16, at)
             quads = tile[:].rearrange("s (h n j) -> s h n j", h=2, j=PACK)
-            return quads, tile[:].bitcast(F32).rearrange("s (h t p u) -> s h t p u", h=2, t=2, u=2)
+            return quads, tile[:].bitcast(F32).rearrange("s (h j p u) -> s h j p u", h=2, j=2, u=2)
+
+        def copy_values(pairs, turned):
+            nc.scalar.copy(pairs, turned.rearrange("s j u (h p) -> s h j p u", h=2))
 
         quarters = [(b, h) for b in range(BLOCKS) for h in range(2)]
         ts_table = keep.tile([P, TOKENS], F32, name="ts_table", align_bytes=64)
@@ -139,26 +135,26 @@ def tile_attend_x_mla_cap_srt_kernel(tc, qT, cT, ts, ch, offs, out):
         nc.scalar.activation(ts_rows[:], ts_table[:].indirect(offsets[:]), ACT.Copy)
 
         k_quads = [keep.tile([P, HALF, PACK], BF16, name=f"k_quads{h}", align_bytes=64) for h in range(2)]
-        k_places = [k_quads[h][:].rearrange("p (s u e) t -> p s u e t", u=2, e=2) for h in range(2)]
+        k_places = [k_quads[h][:].rearrange("p (s u e) j -> p s u e j", u=2, e=2) for h in range(2)]
         pair = shared.tile([P, 2, 2, P, 2], BF16, name="pair", align_bytes=64, offset=PAIR_AT)
         gather(0, pair[:, 0])
-
-        v_early, v_early_words = value_words("v_early", None)
+        v_early, v_early_pairs = value_tile("v_early", None)
         gather_halves(1, pair[:, 1])
         turned_early = psum.tile([P, 2, 2, P], F32, name="turned_early", tag="bank_a2")
-        for t in range(2):
-            turn(pair[:, t], turned_early[:, t])
-        copy_values(v_early_words, turned_early[:])
+        for j in range(2):
+            turn(pair[:, j], turned_early[:, j])
+        copy_values(v_early_pairs, turned_early[:])
         ts_turned = psum.tile([P, PACK, P], F32, name="ts_turned", tag="bank_a1")
         for t in range(PACK):
             nc.tensor.transpose(ts_turned[:, t, :], ts_rows[:].rearrange("q (s t) -> q t s", t=PACK)[:, t], ident[:])
-        pair_halves = pair[:].rearrange("p t u (h s) e -> p h s u e t", h=2)
+        pair_halves = pair[:].rearrange("p j u (h s) e -> p h s u e j", h=2)
         for h in range(2):
             nc.vector.tensor_copy(k_places[h][:, :, :, :, 0:2], pair_halves[:, h])
         third = keep.tile([P, 2, P, 2], BF16, name="third", align_bytes=64)
         gather_halves(2, third[:])
+        third_halves = third[:].rearrange("p u (h s) e -> p h s u e", h=2)
         for h in range(2):
-            nc.vector.tensor_copy(k_places[h][:, :, :, :, 2], halves(third[:])[:, h])
+            nc.vector.tensor_copy(k_places[h][:, :, :, :, 2], third_halves[:, h])
         turned_late = psum.tile([P, 2, 2, P], F32, name="turned_late", tag="bank_a2")
         turn(third[:], turned_late[:, 0])
         last = shared.tile([P, SLOTS], BF16, name="last", align_bytes=64, offset=PAIR_AT)
@@ -173,18 +169,16 @@ def tile_attend_x_mla_cap_srt_kernel(tc, qT, cT, ts, ch, offs, out):
             nc.tensor.transpose(turned_late[:, 1, u, :], last_words[:, u, :], ident[:])
 
         q_quads = []
-        for b in range(BLOCKS):
-            q_quads.append(
-                shared.tile([P, P, PACK], BF16, name=f"q_quads{b}", align_bytes=64, offset=(PAIR_AT + KIB, LAST_PLANE_AT)[b])
-            )
+        for b, at in enumerate((PAIR_AT + KIB, LAST_PLANE_AT)):
+            q_quads.append(shared.tile([P, P, PACK], BF16, name=f"q_quads{b}", align_bytes=64, offset=at))
             nc.scalar.copy(
                 q_quads[b][:].rearrange("p (c i) j -> p c j i", i=PACK),
                 q_raw[:, :, b * P : (b + 1) * P].rearrange("p j (c i) -> p c j i", i=PACK),
             )
         ts_column = place("ts_column", PACK, F32, TS_COLUMN_AT)
         nc.scalar.copy(ts_column[:], ts_turned[:, :, 0])
-        v_late, v_late_words = value_words("v_late", V_LATE_AT)
-        copy_values(v_late_words, turned_late[:])
+        v_late, v_late_pairs = value_tile("v_late", V_LATE_AT)
+        copy_values(v_late_pairs, turned_late[:])
 
         keys = [operand(f"k{h}", HALF, LAST_PLANE_AT + KIB * (h + 1)) for h in range(2)]
         queries = [operand(f"q{b}", P, LAST_PLANE_AT + KIB * (b + 3)) for b in range(BLOCKS)]
@@ -206,17 +200,18 @@ def tile_attend_x_mla_cap_srt_kernel(tc, qT, cT, ts, ch, offs, out):
                 scaled = shared.tile([P, HALF], F32, name="scaled00", align_bytes=64, offset=FIRST_SCALED_AT)
             else:
                 scaled = keep.tile([P, HALF], F32, name=f"scaled{b}{h}")
-            part = slice(h * P // 2, (h + 1) * P // 2)
-            nc.vector.tensor_tensor(scaled[:], scores[b, h][:], ts_rows[:, h * HALF : (h + 1) * HALF], ALU.mult)
-            nc.scalar.activation(
-                capped[b][:].rearrange("q t s -> q s t")[:, part],
-                scaled[:].rearrange("q (s t) -> q s t", t=PACK),
-                ACT.Tanh,
-                scale=1.0 / CAP,
-            )
+            cuts = (0, HALF // 2, HALF) if b == 0 else (0, HALF)
+            for lo, hi in zip(cuts, cuts[1:]):
+                first, end = h * HALF + lo, h * HALF + hi
+                nc.vector.tensor_tensor(scaled[:, lo:hi], scores[b, h][:, lo:hi], ts_rows[:, first:end], ALU.mult)
+                nc.scalar.activation(
+                    capped[b][:].rearrange("q t s -> q s t")[:, first // PACK : end // PACK],
+                    scaled[:, lo:hi].rearrange("q (s t) -> q s t", t=PACK),
+                    ACT.Tanh,
+                    scale=1.0 / CAP,
+                )
         minus_c, minus_m = [], []
-        for b in range(BLOCKS):
-            at = (None, LAST_MINUS_C_AT)[b]
+        for b, at in enumerate((None, LAST_MINUS_C_AT)):
             minus_c.append(place(f"minus_c{b}", SLOTS, F32, at)[:].rearrange("q (t s) -> q t s", t=PACK))
             minus_m.append(keep.tile([P, 1], F32, name=f"minus_m{b}"))
             nc.vector.tensor_scalar(
@@ -226,12 +221,11 @@ def tile_attend_x_mla_cap_srt_kernel(tc, qT, cT, ts, ch, offs, out):
         for h in range(2):
             for n, quads in enumerate((v_early, v_late)):
                 quantize(values[h], quads[:, h], slice(n * P, (n + 1) * P))
-        parts = ((0, 2), (2, 3), (3, 4))
-        total = keep.tile([P, BLOCKS, len(parts)], F32, name="total")
+        total = keep.tile([P, BLOCKS, len(EXP_PARTS)], F32, name="total")
         p_turned = []
         for b in range(BLOCKS):
             p_turned.append(psum.tile([P, PACK, P], F32, name=f"p_turned{b}", tag=f"bank_a{b}"))
-            for n, (lo, hi) in enumerate(parts):
+            for n, (lo, hi) in enumerate(EXP_PARTS):
                 prob = keep.tile([P, hi - lo, P], F32, name=f"prob{b}{n}")
                 nc.scalar.activation(
                     prob[:],
@@ -273,16 +267,16 @@ def tile_attend_x_mla_cap_srt_kernel(tc, qT, cT, ts, ch, offs, out):
         y = {}
         for b, h in quarters:
             y[b, h] = psum.tile([P, PACK, P // 2], F32, name=f"y{b}{h}", tag=f"bank_b{b}{h}")
-            product(y[b, h][:].rearrange("q t p -> q (t p)"), weights[b], values[h])
+            product(y[b, h][:].rearrange("q j p -> q (j p)"), weights[b], values[h])
 
         results = [place("result0", FEATURES, F32, TS_COLUMN_AT), place("result1", FEATURES, F32, None)]
         for b, h in quarters:
             columns = slice(h * HALF, (h + 1) * HALF)
             nc.vector.scalar_tensor_tensor(
-                results[b][:, columns].rearrange("q (p t) -> q p t", t=PACK),
-                y[b, h][:].rearrange("q t p -> q p t"),
+                results[b][:, columns].rearrange("q (p j) -> q p j", j=PACK),
+                y[b, h][:].rearrange("q j p -> q p j"),
                 inverse[:, b : b + 1],
-                channel[:, columns].rearrange("q (p t) -> q p t", t=PACK),
+                channel[:, columns].rearrange("q (p j) -> q p j", j=PACK),
                 ALU.mult,
                 ALU.mult,
             )

@@ -26,16 +26,17 @@ CAP = 2.0
 EXP_PARTS = ((0, 2), (2, 3), (3, 4))
 
 KIB = 1024
-LAST_CAPPED_AT = 0
-LAST_MINUS_C_AT = 4 * KIB
+CAPPED1_AT = 0
+MINUS_C1_AT = 4 * KIB
 PLANES_AT = 8 * KIB
 LAST_PLANE_AT = PLANES_AT + 3 * 8 * KIB
 Q_RAW_AT = 42 * KIB
 V_LATE_AT = Q_RAW_AT
 FIRST_SCALED_AT = V_LATE_AT + 2 * KIB
-TS_COLUMN_AT = FIRST_SCALED_AT + KIB
+TS_COLUMN_AT = V_LATE_AT + 3 * KIB
 PAIR_AT = 48 * KIB
-
+Q_QUADS0_AT = PAIR_AT + KIB
+Q_QUADS1_AT = 52 * KIB
 SPREAD_BANKS = ("bank_b00", "bank_b01", "bank_b10", "bank_a2")
 
 FLOPS = 2 * 2 * QUERIES * SLOTS * FEATURES
@@ -48,36 +49,13 @@ def tile_attend_x_mla_cap_srt_kernel(tc, qT, cT, ts, ch, offs, out):
         shared = ctx.enter_context(tc.tile_pool(name="shared", bufs=1))
         psum = ctx.enter_context(tc.psum_pool(name="psum", bufs=1))
 
-        ts_runs = keep.tile([P, RUN], F32, name="ts_runs")
-        nc.scalar.dma_start(ts_runs[:], ts[0].rearrange("(p j) -> p j", j=RUN))
-        offsets = keep.tile([P, SLOTS // LIST_ROWS], U16, name="offsets")
-        plane_rows = cT.rearrange("(p j) w -> j p w", j=PACK)
-        planes = [
-            shared.tile([P, TOKENS], F32, name=f"plane{j}", align_bytes=64, offset=PLANES_AT + 8 * KIB * j)
-            for j in range(PACK)
-        ]
-        nc.sync.dma_start(planes[0][:], plane_rows[0])
-        nc.sync.dma_start(offsets[:], offs)
-        for j in (1, 2, 3):
-            nc.sync.dma_start(planes[j][:], plane_rows[j])
-        q_raw = shared.tile([P, PACK, QUERIES], F32, name="q_raw", align_bytes=64, offset=Q_RAW_AT)
-        nc.sync.dma_start(q_raw[:], qT[0].rearrange("(p j) q -> p j q", j=PACK))
-        channel = keep.tile([P, FEATURES], F32, name="channel")
-        nc.sync.dma_start(channel[:], ch)
-
-        ident = keep.tile([P, P], F32, name="ident")
-        make_identity(nc, ident[:])
-        warm = keep.tile([P, 1], F32, name="warm")
-        nc.gpsimd.memset(warm[:], 0.0)
-        nc.scalar.activation(warm[:], warm[:], ACT.Exp)
-
-        def place(name, width, dtype, at):
+        def place(name, shape, dtype, at=None):
             if at is None:
-                return keep.tile([P, width], dtype, name=name, align_bytes=64)
-            return shared.tile([P, width], dtype, name=name, align_bytes=64, offset=at)
+                return keep.tile(shape, dtype, name=name, align_bytes=64)
+            return shared.tile(shape, dtype, name=name, align_bytes=64, offset=at)
 
         def operand(name, width, codes_at=None, scales_at=None):
-            return place(f"{name}_codes", width, U32, codes_at), place(f"{name}_scales", width, U8, scales_at)
+            return place(f"{name}_codes", [P, width], U32, codes_at), place(f"{name}_scales", [P, width], U8, scales_at)
 
         def quantize(target, quads, columns=slice(None)):
             nc.vector.quantize_mx(
@@ -86,42 +64,43 @@ def tile_attend_x_mla_cap_srt_kernel(tc, qT, cT, ts, ch, offs, out):
                 in_=quads.rearrange("p n j -> p (n j)"),
             )
 
-        def product(result, stationary, moving):
+        def product(result, stationary, moving, columns=slice(None)):
             nc.tensor.matmul_mx(
                 out=result,
                 lhsT=stationary[0][:].bitcast(FP8X4),
                 lhsT_scale=stationary[1][:],
-                rhs=moving[0][:].bitcast(FP8X4),
-                rhs_scale=moving[1][:],
+                rhs=moving[0][:, columns].bitcast(FP8X4),
+                rhs_scale=moving[1][:, columns],
                 start=True,
                 stop=True,
             )
 
-        def gather(j, picked):
-            nc.vector.tensor_copy(picked.rearrange("p u s e -> p s u e"), planes[j][:].indirect(offsets[:]))
+        ts_runs = place("ts_runs", [P, RUN], F32)
+        nc.scalar.dma_start(ts_runs[:], ts[0].rearrange("(p j) -> p j", j=RUN))
+        offsets = keep.tile([P, SLOTS // LIST_ROWS], U16, name="offsets")
+        plane_rows = cT.rearrange("(p j) w -> j p w", j=PACK)
+        planes = [place(f"plane{j}", [P, TOKENS], F32, PLANES_AT + 8 * KIB * j) for j in range(PACK)]
+        nc.sync.dma_start(planes[0][:], plane_rows[0])
+        nc.sync.dma_start(offsets[:], offs)
+        for j in (1, 2, 3):
+            nc.sync.dma_start(planes[j][:], plane_rows[j])
+        q_raw = place("q_raw", [P, PACK, QUERIES], F32, Q_RAW_AT)
+        q_rows = qT[0].rearrange("(p j) q -> p j q", j=PACK)
+        for a in range(2):
+            nc.sync.dma_start(q_raw[:, 2 * a : 2 * a + 2], q_rows[:, 2 * a : 2 * a + 2])
+        channel = place("channel", [P, FEATURES], F32)
+        nc.sync.dma_start(channel[:], ch)
 
-        def gather_halves(j, picked):
-            for h in range(2):
-                nc.vector.tensor_copy(
-                    picked.rearrange("p u s e -> p s u e")[:, h * P // 2 : (h + 1) * P // 2],
-                    planes[j][:].indirect(offsets[:, h * HALF // LIST_ROWS : (h + 1) * HALF // LIST_ROWS]),
-                )
+        ident = place("ident", [P, P], F32)
+        make_identity(nc, ident[:])
+        warm = keep.tile([P, 1], F32, name="warm")
+        nc.gpsimd.memset(warm[:], 0.0)
+        nc.scalar.activation(warm[:], warm[:], ACT.Exp)
 
-        def turn(picked, turned):
-            words = picked.rearrange("p u s e -> p u (s e)").bitcast(F32)
-            for u in range(2):
-                nc.tensor.transpose(turned[:, u, :], words[:, u, :], ident[:])
+        def listed(window, first, end):
+            return window[:].indirect(offsets[:, first // LIST_ROWS : end // LIST_ROWS])
 
-        def value_tile(name, at):
-            tile = place(name, 2 * P * PACK, BF16, at)
-            quads = tile[:].rearrange("s (h n j) -> s h n j", h=2, j=PACK)
-            return quads, tile[:].bitcast(F32).rearrange("s (h j p u) -> s h j p u", h=2, j=2, u=2)
-
-        def copy_values(pairs, turned):
-            nc.scalar.copy(pairs, turned.rearrange("s j u (h p) -> s h j p u", h=2))
-
-        quarters = [(b, h) for b in range(BLOCKS) for h in range(2)]
-        ts_table = keep.tile([P, TOKENS], F32, name="ts_table", align_bytes=64)
+        ts_table = place("ts_table", [P, TOKENS], F32)
         for n in range(RUN // PACK):
             spread = psum.tile([P, PACK, P], F32, name=f"spread{n}", tag=SPREAD_BANKS[n])
             for j in range(PACK):
@@ -131,18 +110,38 @@ def tile_attend_x_mla_cap_srt_kernel(tc, qT, cT, ts, ch, offs, out):
                 ts_table[:].rearrange("q (p j) -> q p j", j=RUN)[:, :, PACK * n : PACK * (n + 1)],
                 spread[:].rearrange("q j p -> q p j"),
             )
-        ts_rows = keep.tile([P, SLOTS], F32, name="ts_rows")
-        nc.scalar.activation(ts_rows[:], ts_table[:].indirect(offsets[:]), ACT.Copy)
+        ts_rows = place("ts_rows", [P, SLOTS], F32)
+        nc.scalar.activation(ts_rows[:], listed(ts_table, 0, SLOTS), ACT.Copy)
 
-        k_quads = [keep.tile([P, HALF, PACK], BF16, name=f"k_quads{h}", align_bytes=64) for h in range(2)]
+        def gather_dealt(j, picked, cuts):
+            dealt = picked.rearrange("p u s e -> p s u e")
+            for first, end in zip(cuts, cuts[1:]):
+                nc.vector.tensor_copy(dealt[:, first // PACK : end // PACK], listed(planes[j], first, end))
+
+        def turn(words, turned):
+            for u in range(2):
+                nc.tensor.transpose(turned[:, u, :], words[:, u, :], ident[:])
+
+        def dealt_words(picked):
+            return picked.rearrange("p u s e -> p u (s e)").bitcast(F32)
+
+        def value_tile(name, at):
+            tile = place(name, [P, 2 * P * PACK], BF16, at)
+            quads = tile[:].rearrange("s (h n j) -> s h n j", h=2, j=PACK)
+            return quads, tile[:].bitcast(F32).rearrange("s (h j p u) -> s h j p u", h=2, j=2, u=2)
+
+        def copy_values(pairs, turned):
+            nc.scalar.copy(pairs, turned.rearrange("s j u (h p) -> s h j p u", h=2))
+
+        k_quads = [place(f"k_quads{h}", [P, HALF, PACK], BF16) for h in range(2)]
         k_places = [k_quads[h][:].rearrange("p (s u e) j -> p s u e j", u=2, e=2) for h in range(2)]
-        pair = shared.tile([P, 2, 2, P, 2], BF16, name="pair", align_bytes=64, offset=PAIR_AT)
-        gather(0, pair[:, 0])
+        pair = place("pair", [P, 2, 2, P, 2], BF16, PAIR_AT)
+        gather_dealt(0, pair[:, 0], (0, SLOTS))
+        gather_dealt(1, pair[:, 1], (0, HALF, SLOTS))
         v_early, v_early_pairs = value_tile("v_early", None)
-        gather_halves(1, pair[:, 1])
         turned_early = psum.tile([P, 2, 2, P], F32, name="turned_early", tag="bank_a2")
         for j in range(2):
-            turn(pair[:, j], turned_early[:, j])
+            turn(dealt_words(pair[:, j]), turned_early[:, j])
         copy_values(v_early_pairs, turned_early[:])
         ts_turned = psum.tile([P, PACK, P], F32, name="ts_turned", tag="bank_a1")
         for t in range(PACK):
@@ -150,74 +149,78 @@ def tile_attend_x_mla_cap_srt_kernel(tc, qT, cT, ts, ch, offs, out):
         pair_halves = pair[:].rearrange("p j u (h s) e -> p h s u e j", h=2)
         for h in range(2):
             nc.vector.tensor_copy(k_places[h][:, :, :, :, 0:2], pair_halves[:, h])
-        third = keep.tile([P, 2, P, 2], BF16, name="third", align_bytes=64)
-        gather_halves(2, third[:])
+        third = place("third", [P, 2, P, 2], BF16)
+        gather_dealt(2, third[:], (0, HALF, SLOTS))
         third_halves = third[:].rearrange("p u (h s) e -> p h s u e", h=2)
         for h in range(2):
             nc.vector.tensor_copy(k_places[h][:, :, :, :, 2], third_halves[:, h])
         turned_late = psum.tile([P, 2, 2, P], F32, name="turned_late", tag="bank_a2")
-        turn(third[:], turned_late[:, 0])
-        last = shared.tile([P, SLOTS], BF16, name="last", align_bytes=64, offset=PAIR_AT)
-        cut = HALF // LIST_ROWS
-        nc.vector.tensor_copy(last[:, :HALF], planes[3][:].indirect(offsets[:, :cut]))
-        nc.scalar.activation(last[:, HALF:], planes[3][:].indirect(offsets[:, cut:]), ACT.Copy)
-        last_halves = last[:].rearrange("p (h s u e) -> p h s u e", h=2, u=2, e=2)
+        turn(dealt_words(third[:]), turned_late[:, 0])
+        last = place("last", [P, SLOTS], BF16, PAIR_AT)
+        nc.vector.tensor_copy(last[:, :HALF], listed(planes[3], 0, HALF))
+        nc.scalar.activation(last[:, HALF:], listed(planes[3], HALF, SLOTS), ACT.Copy)
         for h in range(2):
-            nc.vector.tensor_copy(k_places[h][:, :, :, :, 3], last_halves[:, h])
-        last_words = last[:].bitcast(F32).rearrange("p (s u) -> p u s", u=2)
-        for u in range(2):
-            nc.tensor.transpose(turned_late[:, 1, u, :], last_words[:, u, :], ident[:])
+            nc.vector.tensor_copy(k_quads[h][:, :, 3], last[:, h * HALF : (h + 1) * HALF])
+        turn(last[:].bitcast(F32).rearrange("p (s u) -> p u s", u=2), turned_late[:, 1])
 
-        q_quads = []
-        for b, at in enumerate((PAIR_AT + KIB, LAST_PLANE_AT)):
-            q_quads.append(shared.tile([P, P, PACK], BF16, name=f"q_quads{b}", align_bytes=64, offset=at))
+        q_quads = [place("q_quads0", [P, P, PACK], BF16, Q_QUADS0_AT), place("q_quads1", [P, P, PACK], BF16, Q_QUADS1_AT)]
+
+        def weave_queries(b, rows):
             nc.scalar.copy(
-                q_quads[b][:].rearrange("p (c i) j -> p c j i", i=PACK),
-                q_raw[:, :, b * P : (b + 1) * P].rearrange("p j (c i) -> p c j i", i=PACK),
+                q_quads[b][:].rearrange("p (c i) j -> p c j i", i=PACK)[:, :, rows],
+                q_raw[:, rows, b * P : (b + 1) * P].rearrange("p j (c i) -> p c j i", i=PACK),
             )
-        ts_column = place("ts_column", PACK, F32, TS_COLUMN_AT)
+
+        weave_queries(0, slice(0, 2))
+        weave_queries(0, slice(2, 4))
+        weave_queries(1, slice(0, 4))
+        ts_column = place("ts_column", [P, PACK], F32, TS_COLUMN_AT)
         nc.scalar.copy(ts_column[:], ts_turned[:, :, 0])
         v_late, v_late_pairs = value_tile("v_late", V_LATE_AT)
         copy_values(v_late_pairs, turned_late[:])
 
-        keys = [operand(f"k{h}", HALF, LAST_PLANE_AT + KIB * (h + 1)) for h in range(2)]
-        queries = [operand(f"q{b}", P, LAST_PLANE_AT + KIB * (b + 3)) for b in range(BLOCKS)]
-        for h in range(2):
-            quantize(keys[h], k_quads[h][:])
-        for b in range(BLOCKS):
-            quantize(queries[b], q_quads[b][:])
-        scores = {}
-        for b, h in quarters:
-            scores[b, h] = psum.tile([P, HALF], F32, name=f"scores{b}{h}", tag=f"bank_b{b}{h}")
-            product(scores[b, h][:], queries[b], keys[h])
-
-        capped = [
-            keep.tile([P, PACK, P], F32, name="capped0"),
-            shared.tile([P, PACK, P], F32, name="capped1", align_bytes=64, offset=LAST_CAPPED_AT),
+        keys = [
+            operand("k0", HALF, LAST_PLANE_AT + KIB),
+            operand("k1", HALF, LAST_PLANE_AT + 2 * KIB, Q_QUADS0_AT),
         ]
+        queries = [operand(f"q{b}", P, LAST_PLANE_AT + KIB * (b + 3)) for b in range(BLOCKS)]
+        quantize(keys[0], k_quads[0][:])
+        quantize(queries[0], q_quads[0][:])
+        quantize(keys[1], k_quads[1][:])
+        quantize(queries[1], q_quads[1][:])
+        quarters = [(b, h) for b in range(BLOCKS) for h in range(2)]
+        scores = {}
+        pieces = [(0, 0, P, "bank_a0"), (0, P, HALF, "bank_b00"), (0, HALF, SLOTS, "bank_b01")]
+        pieces += [(1, 0, HALF, "bank_b10"), (1, HALF, SLOTS, "bank_b11")]
+        for b, first, end, bank in pieces:
+            h, lo = divmod(first, HALF)
+            scores[b, first] = psum.tile([P, end - first], F32, name=f"scores{b}_{first}", tag=bank)
+            product(scores[b, first][:], queries[b], keys[h], slice(lo, lo + end - first))
+
+        capped = [place("capped0", [P, PACK, P], F32), place("capped1", [P, PACK, P], F32, CAPPED1_AT)]
+        scaled = {}
         for b, h in quarters:
-            if (b, h) == quarters[0]:
-                scaled = shared.tile([P, HALF], F32, name="scaled00", align_bytes=64, offset=FIRST_SCALED_AT)
-            else:
-                scaled = keep.tile([P, HALF], F32, name=f"scaled{b}{h}")
+            scaled[b, h] = place(f"scaled{b}{h}", [P, HALF], F32, FIRST_SCALED_AT if (b, h) == quarters[0] else None)
             cuts = (0, HALF // 2, HALF) if b == 0 else (0, HALF)
             for lo, hi in zip(cuts, cuts[1:]):
                 first, end = h * HALF + lo, h * HALF + hi
-                nc.vector.tensor_tensor(scaled[:, lo:hi], scores[b, h][:, lo:hi], ts_rows[:, first:end], ALU.mult)
+                start = first if (b, first) in scores else h * HALF
+                source = scores[b, start][:, first - start : end - start]
+                nc.vector.tensor_tensor(scaled[b, h][:, lo:hi], source, ts_rows[:, first:end], ALU.mult)
                 nc.scalar.activation(
                     capped[b][:].rearrange("q t s -> q s t")[:, first // PACK : end // PACK],
-                    scaled[:, lo:hi].rearrange("q (s t) -> q s t", t=PACK),
+                    scaled[b, h][:, lo:hi].rearrange("q (s t) -> q s t", t=PACK),
                     ACT.Tanh,
                     scale=1.0 / CAP,
                 )
         minus_c, minus_m = [], []
-        for b, at in enumerate((None, LAST_MINUS_C_AT)):
-            minus_c.append(place(f"minus_c{b}", SLOTS, F32, at)[:].rearrange("q (t s) -> q t s", t=PACK))
+        for b, at in enumerate((None, MINUS_C1_AT)):
+            minus_c.append(place(f"minus_c{b}", [P, PACK, P], F32, at))
             minus_m.append(keep.tile([P, 1], F32, name=f"minus_m{b}"))
             nc.vector.tensor_scalar(
-                minus_c[b], capped[b][:], -CAP, None, ALU.mult, ALU.min, accum_out=minus_m[b][:]
+                minus_c[b][:], capped[b][:], -CAP, None, ALU.mult, ALU.min, accum_out=minus_m[b][:]
             )
-        values = [operand(f"v{h}", HALF, scales_at=LAST_CAPPED_AT + HALF * h) for h in range(2)]
+        values = [operand(f"v{h}", HALF, scales_at=CAPPED1_AT + HALF * h) for h in range(2)]
         for h in range(2):
             for n, quads in enumerate((v_early, v_late)):
                 quantize(values[h], quads[:, h], slice(n * P, (n + 1) * P))
@@ -237,13 +240,13 @@ def tile_attend_x_mla_cap_srt_kernel(tc, qT, cT, ts, ch, offs, out):
                 )
                 for t in range(lo, hi):
                     nc.tensor.transpose(p_turned[b][:, t, :], prob[:, t - lo, :], ident[:])
-        part_sum = place("part_sum", BLOCKS, F32, LAST_MINUS_C_AT)
+        part_sum = place("part_sum", [P, BLOCKS], F32, MINUS_C1_AT)
         row_sum = keep.tile([P, BLOCKS], F32, name="row_sum")
         for b in range(BLOCKS):
             nc.scalar.activation(part_sum[:, b : b + 1], total[:, b, 0:1], ACT.Identity, bias=total[:, b, 1:2])
         for b in range(BLOCKS):
             nc.scalar.activation(row_sum[:, b : b + 1], part_sum[:, b : b + 1], ACT.Identity, bias=total[:, b, 2:3])
-        w_quads = [keep.tile([P, P, PACK], BF16, name=f"w_quads{b}", align_bytes=64) for b in range(BLOCKS)]
+        w_quads = [place(f"w_quads{b}", [P, P, PACK], BF16) for b in range(BLOCKS)]
         weights = [operand(f"w{b}", P) for b in range(BLOCKS)]
 
         def weigh(b, lo, hi):
@@ -269,7 +272,7 @@ def tile_attend_x_mla_cap_srt_kernel(tc, qT, cT, ts, ch, offs, out):
             y[b, h] = psum.tile([P, PACK, P // 2], F32, name=f"y{b}{h}", tag=f"bank_b{b}{h}")
             product(y[b, h][:].rearrange("q j p -> q (j p)"), weights[b], values[h])
 
-        results = [place("result0", FEATURES, F32, TS_COLUMN_AT), place("result1", FEATURES, F32, None)]
+        results = [place("result0", [P, FEATURES], F32, TS_COLUMN_AT), place("result1", [P, FEATURES], F32)]
         for b, h in quarters:
             columns = slice(h * HALF, (h + 1) * HALF)
             nc.vector.scalar_tensor_tensor(

@@ -51,8 +51,8 @@ def tile_attend_x_mla_cap_srt_kernel(tc, qT, cT, ts, ch, offs, out):
 
         def place(name, shape, dtype, at=None):
             if at is None:
-                return keep.tile(shape, dtype, name=name, align_bytes=64)
-            return shared.tile(shape, dtype, name=name, align_bytes=64, offset=at)
+                return keep.tile(shape, dtype, name=name, align_bytes=256)
+            return shared.tile(shape, dtype, name=name, align_bytes=256, offset=at)
 
         def operand(name, width, codes_at=None, scales_at=None):
             return place(f"{name}_codes", [P, width], U32, codes_at), place(f"{name}_scales", [P, width], U8, scales_at)
@@ -144,8 +144,10 @@ def tile_attend_x_mla_cap_srt_kernel(tc, qT, cT, ts, ch, offs, out):
             turn(dealt_words(pair[:, j]), turned_early[:, j])
         copy_values(v_early_pairs, turned_early[:])
         ts_turned = psum.tile([P, PACK, P], F32, name="ts_turned", tag="bank_a1")
+        ts_dealt = place("ts_dealt", [P, PACK, P], F32)
+        nc.scalar.copy(ts_dealt[:].rearrange("q t s -> q s t"), ts_rows[:].rearrange("q (s t) -> q s t", t=PACK))
         for t in range(PACK):
-            nc.tensor.transpose(ts_turned[:, t, :], ts_rows[:].rearrange("q (s t) -> q t s", t=PACK)[:, t], ident[:])
+            nc.tensor.transpose(ts_turned[:, t, :], ts_dealt[:, t], ident[:])
         pair_halves = pair[:].rearrange("p j u (h s) e -> p h s u e j", h=2)
         for h in range(2):
             nc.vector.tensor_copy(k_places[h][:, :, :, :, 0:2], pair_halves[:, h])

@@ -75,8 +75,10 @@ def tile_attend_x_mla_cap_srt_kernel(tc, qT, cT, ts, ch, offs, out):
                 stop=True,
             )
 
-        ts_runs = place("ts_runs", [P, RUN], F32)
-        nc.scalar.dma_start(ts_runs[:], ts[0].rearrange("(p j) -> p j", j=RUN))
+        ts_lines = place("ts_lines", [P, P], F32)
+        nc.scalar.dma_start(ts_lines[RUN : 2 * RUN], ts[0].rearrange("(r c) -> r c", c=P))
+        for first, end in ((0, RUN), (2 * RUN, P // 2), (P // 2, P)):
+            nc.gpsimd.memset(ts_lines[first:end], 0.0)
         offsets = keep.tile([P, SLOTS // LIST_ROWS], U16, name="offsets")
         plane_rows = cT.rearrange("(p j) w -> j p w", j=PACK)
         planes = [place(f"plane{j}", [P, TOKENS], F32, PLANES_AT + 8 * KIB * j) for j in range(PACK)]
@@ -101,15 +103,16 @@ def tile_attend_x_mla_cap_srt_kernel(tc, qT, cT, ts, ch, offs, out):
             return window[:].indirect(offsets[:, first // LIST_ROWS : end // LIST_ROWS])
 
         ts_table = place("ts_table", [P, TOKENS], F32)
+        ts_down = psum.tile([P, P], F32, name="ts_down", tag="bank_a0")
+        nc.tensor.transpose(ts_down[:], ts_lines[:], ident[:])
+        ts_runs = place("ts_runs", [P, RUN], F32)
+        nc.scalar.copy(ts_runs[:], ts_down[:, RUN : 2 * RUN])
         for n in range(RUN // PACK):
             spread = psum.tile([P, PACK, P], F32, name=f"spread{n}", tag=SPREAD_BANKS[n])
             for j in range(PACK):
                 column = ts_runs[:, PACK * n + j : PACK * n + j + 1]
                 nc.tensor.transpose(spread[:, j, :], column.to_broadcast([P, P]), ident[:])
-            nc.scalar.copy(
-                ts_table[:].rearrange("q (p j) -> q p j", j=RUN)[:, :, PACK * n : PACK * (n + 1)],
-                spread[:].rearrange("q j p -> q p j"),
-            )
+            nc.scalar.copy(ts_table[:, n * PACK * P : (n + 1) * PACK * P], spread[:].rearrange("q j p -> q (j p)"))
         ts_rows = place("ts_rows", [P, SLOTS], F32)
         nc.scalar.activation(ts_rows[:], listed(ts_table, 0, SLOTS), ACT.Copy)
 

@@ -191,11 +191,12 @@ def tile_attend_x_mla_cap_srt_kernel(tc, qT, cT, ts, ch, offs, out):
         queries = [operand(f"q{b}", P, LAST_PLANE_AT + KIB * (b + 3)) for b in range(BLOCKS)]
         quantize(keys[0], k_quads[0][:])
         quantize(queries[0], q_quads[0][:])
-        quantize(keys[1], k_quads[1][:])
+        for lo in (0, P):
+            quantize(keys[1], k_quads[1][:, lo : lo + P], slice(lo, lo + P))
         quantize(queries[1], q_quads[1][:])
         quarters = [(b, h) for b in range(BLOCKS) for h in range(2)]
         scores = {}
-        pieces = [(0, 0, P, "bank_a0"), (0, P, HALF, "bank_b00"), (0, HALF, SLOTS, "bank_b01")]
+        pieces = [(0, 0, P, "bank_a0"), (0, P, HALF, "bank_b00"), (0, HALF, HALF + P, "bank_a3"), (0, HALF + P, SLOTS, "bank_b01")]
         pieces += [(1, 0, HALF, "bank_b10"), (1, HALF, SLOTS, "bank_b11")]
         for b, first, end, bank in pieces:
             h, lo = divmod(first, HALF)

@@ -197,7 +197,7 @@ def tile_attend_x_mla_cap_srt_kernel(tc, qT, cT, ts, ch, offs, out):
         quarters = [(b, h) for b in range(BLOCKS) for h in range(2)]
         scores = {}
         pieces = [(0, 0, P, "bank_a0"), (0, P, HALF, "bank_b00"), (0, HALF, HALF + P, "bank_a3"), (0, HALF + P, SLOTS, "bank_b01")]
-        pieces += [(1, 0, HALF, "bank_b10"), (1, HALF, SLOTS, "bank_b11")]
+        pieces += [(1, 0, HALF, "bank_b10"), (1, HALF, HALF + P, "bank_b11"), (1, HALF + P, SLOTS, "bank_a1")]
         for b, first, end, bank in pieces:
             h, lo = divmod(first, HALF)
             scores[b, first] = psum.tile([P, end - first], F32, name=f"scores{b}_{first}", tag=bank)
@@ -207,7 +207,7 @@ def tile_attend_x_mla_cap_srt_kernel(tc, qT, cT, ts, ch, offs, out):
         scaled = {}
         for b, h in quarters:
             scaled[b, h] = place(f"scaled{b}{h}", [P, HALF], F32, FIRST_SCALED_AT if (b, h) == quarters[0] else None)
-            cuts = (0, HALF // 2, HALF) if b == 0 else (0, HALF)
+            cuts = (0, HALF) if (b, h) == (1, 0) else (0, HALF // 2, HALF)
             for lo, hi in zip(cuts, cuts[1:]):
                 first, end = h * HALF + lo, h * HALF + hi
                 start = first if (b, first) in scores else h * HALF

@@ -140,7 +140,7 @@ def tile_attend_x_mla_cap_srt_kernel(tc, qT, cT, ts, ch, offs, out):
         k_places = [k_quads[h][:].rearrange("p (s u e) j -> p s u e j", u=2, e=2) for h in range(2)]
         pair = place("pair", [P, 2, 2, P, 2], BF16, PAIR_AT)
         gather_dealt(0, pair[:, 0], (0, SLOTS))
-        gather_dealt(1, pair[:, 1], (0, HALF, SLOTS))
+        gather_dealt(1, pair[:, 1], (0, SLOTS))
         v_early, v_early_pairs = value_tile("v_early", None)
         turned_early = psum.tile([P, 2, 2, P], F32, name="turned_early", tag="bank_a2")
         for j in range(2):
@@ -155,7 +155,7 @@ def tile_attend_x_mla_cap_srt_kernel(tc, qT, cT, ts, ch, offs, out):
         for h in range(2):
             nc.vector.tensor_copy(k_places[h][:, :, :, :, 0:2], pair_halves[:, h])
         third = place("third", [P, 2, P, 2], BF16)
-        gather_dealt(2, third[:], (0, HALF, SLOTS))
+        gather_dealt(2, third[:], (0, SLOTS))
         third_halves = third[:].rearrange("p u (h s) e -> p h s u e", h=2)
         for h in range(2):
             nc.vector.tensor_copy(k_places[h][:, :, :, :, 2], third_halves[:, h])

from contextlib import ExitStack

import concourse.mybir as mybir
from concourse.masks import make_identity

F32 = mybir.dt.float32
BF16 = mybir.dt.bfloat16
U32 = mybir.dt.uint32
U16 = mybir.dt.uint16
U8 = mybir.dt.uint8
FP8X4 = mybir.dt.float8_e4m3fn_x4
ACT = mybir.ActivationFunctionType
ALU = mybir.AluOpType

P = 128
PACK = 4
TOKENS = 2048
SLOTS = 512
QUERIES = 256
FEATURES = 512
BLOCKS = QUERIES // P
HALF = SLOTS // 2
LIST_ROWS = 16
RUN = TOKENS // P
CAP = 2.0
EXP_PARTS = ((0, 2), (2, 3), (3, 4))

KIB = 1024
CAPPED1_AT = 0
MINUS_C1_AT = 4 * KIB
PLANES_AT = 8 * KIB
LAST_PLANE_AT = PLANES_AT + 3 * 8 * KIB
Q_RAW_AT = 42 * KIB
V_LATE_AT = Q_RAW_AT
FIRST_SCALED_AT = V_LATE_AT + 2 * KIB
TS_COLUMN_AT = V_LATE_AT + 3 * KIB
PAIR_AT = 48 * KIB
Q_QUADS0_AT = PAIR_AT + KIB
Q_QUADS1_AT = 52 * KIB
SPREAD_BANKS = ("bank_b00", "bank_b01", "bank_b10", "bank_a2")

FLOPS = 2 * 2 * QUERIES * SLOTS * FEATURES


def tile_attend_x_mla_cap_srt_kernel(tc, qT, cT, ts, ch, offs, out):
    nc = tc.nc
    with ExitStack() as ctx:
        keep = ctx.enter_context(tc.tile_pool(name="keep", bufs=1))
        shared = ctx.enter_context(tc.tile_pool(name="shared", bufs=1))
        psum = ctx.enter_context(tc.psum_pool(name="psum", bufs=1))

        def place(name, shape, dtype, at=None):
            if at is None:
                return keep.tile(shape, dtype, name=name, align_bytes=256)
            return shared.tile(shape, dtype, name=name, align_bytes=256, offset=at)

        def operand(name, width, codes_at=None, scales_at=None):
            return place(f"{name}_codes", [P, width], U32, codes_at), place(f"{name}_scales", [P, width], U8, scales_at)

        def quantize(target, quads, columns=slice(None)):
            nc.vector.quantize_mx(
                out=target[0][:, columns].bitcast(FP8X4),
                scales=target[1][:, columns],
                in_=quads.rearrange("p n j -> p (n j)"),
            )

        def product(result, stationary, moving, columns=slice(None)):
            nc.tensor.matmul_mx(
                out=result,
                lhsT=stationary[0][:].bitcast(FP8X4),
                lhsT_scale=stationary[1][:],
                rhs=moving[0][:, columns].bitcast(FP8X4),
                rhs_scale=moving[1][:, columns],
                start=True,
                stop=True,
            )

        ts_lines = place("ts_lines", [P, P], F32)
        nc.scalar.dma_start(ts_lines[RUN : 2 * RUN], ts[0].rearrange("(r c) -> r c", c=P))
        for first, end in ((0, RUN), (2 * RUN, P // 2), (P // 2, P)):
            nc.gpsimd.memset(ts_lines[first:end], 0.0)
        offsets = keep.tile([P, SLOTS // LIST_ROWS], U16, name="offsets")
        plane_rows = cT.rearrange("(p j) w -> j p w", j=PACK)
        planes = [place(f"plane{j}", [P, TOKENS], F32, PLANES_AT + 8 * KIB * j) for j in range(PACK)]
        nc.sync.dma_start(planes[0][:], plane_rows[0])
        nc.sync.dma_start(offsets[:], offs)
        for j in (1, 2, 3):
            nc.sync.dma_start(planes[j][:], plane_rows[j])
        q_raw = place("q_raw", [P, PACK, QUERIES], F32, Q_RAW_AT)
        q_rows = qT[0].rearrange("(p j) q -> p j q", j=PACK)
        for a in range(2):
            nc.sync.dma_start(q_raw[:, 2 * a : 2 * a + 2], q_rows[:, 2 * a : 2 * a + 2])
        channel = place("channel", [P, FEATURES], F32)
        nc.sync.dma_start(channel[:], ch)

        ident = place("ident", [P, P], F32)
        make_identity(nc, ident[:])
        warm = keep.tile([P, 1], F32, name="warm")
        nc.gpsimd.memset(warm[:], 0.0)
        nc.scalar.activation(warm[:], warm[:], ACT.Exp)

        def listed(window, first, end):
            return window[:].indirect(offsets[:, first // LIST_ROWS : end // LIST_ROWS])

        ts_table = place("ts_table", [P, TOKENS], F32)
        ts_down = psum.tile([P, P], F32, name="ts_down", tag="bank_a0")
        nc.tensor.transpose(ts_down[:], ts_lines[:], ident[:])
        ts_runs = place("ts_runs", [P, RUN], F32)
        nc.scalar.copy(ts_runs[:], ts_down[:, RUN : 2 * RUN])
        for n in range(RUN // PACK):
            spread = psum.tile([P, PACK, P], F32, name=f"spread{n}", tag=SPREAD_BANKS[n])
            for j in range(PACK):
                column = ts_runs[:, PACK * n + j : PACK * n + j + 1]
                nc.tensor.transpose(spread[:, j, :], column.to_broadcast([P, P]), ident[:])
            nc.scalar.copy(ts_table[:, n * PACK * P : (n + 1) * PACK * P], spread[:].rearrange("q j p -> q (j p)"))
        ts_rows = place("ts_rows", [P, SLOTS], F32)
        nc.scalar.activation(ts_rows[:], listed(ts_table, 0, SLOTS), ACT.Copy)

        def gather_dealt(j, picked, cuts):
            dealt = picked.rearrange("p u s e -> p s u e")
            for first, end in zip(cuts, cuts[1:]):
                nc.vector.tensor_copy(dealt[:, first // PACK : end // PACK], listed(planes[j], first, end))

        def turn(words, turned):
            for u in range(2):
                nc.tensor.transpose(turned[:, u, :], words[:, u, :], ident[:])

        def dealt_words(picked):
            return picked.rearrange("p u s e -> p u (s e)").bitcast(F32)

        def value_tile(name, at):
            tile = place(name, [P, 2 * P * PACK], BF16, at)
            quads = tile[:].rearrange("s (h n j) -> s h n j", h=2, j=PACK)
            return quads, tile[:].bitcast(F32).rearrange("s (h j p u) -> s h j p u", h=2, j=2, u=2)

        def copy_values(pairs, turned):
            nc.scalar.copy(pairs, turned.rearrange("s j u (h p) -> s h j p u", h=2))

        k_quads = [place(f"k_quads{h}", [P, HALF, PACK], BF16) for h in range(2)]
        k_places = [k_quads[h][:].rearrange("p (s u e) j -> p s u e j", u=2, e=2) for h in range(2)]
        pair = place("pair", [P, 2, 2, P, 2], BF16, PAIR_AT)
        gather_dealt(0, pair[:, 0], (0, SLOTS))
        gather_dealt(1, pair[:, 1], (0, SLOTS))
        v_early, v_early_pairs = value_tile("v_early", None)
        turned_early = psum.tile([P, 2, 2, P], F32, name="turned_early", tag="bank_a2")
        for j in range(2):
            turn(dealt_words(pair[:, j]), turned_early[:, j])
        copy_values(v_early_pairs, turned_early[:])
        ts_turned = psum.tile([P, PACK, P], F32, name="ts_turned", tag="bank_a1")
        ts_dealt = place("ts_dealt", [P, PACK, P], F32)
        nc.scalar.copy(ts_dealt[:].rearrange("q t s -> q s t"), ts_rows[:].rearrange("q (s t) -> q s t", t=PACK))
        for t in range(PACK):
            nc.tensor.transpose(ts_turned[:, t, :], ts_dealt[:, t], ident[:])
        pair_halves = pair[:].rearrange("p j u (h s) e -> p h s u e j", h=2)
        for h in range(2):
            nc.vector.tensor_copy(k_places[h][:, :, :, :, 0:2], pair_halves[:, h])
        third = place("third", [P, 2, P, 2], BF16)
        gather_dealt(2, third[:], (0, SLOTS))
        third_halves = third[:].rearrange("p u (h s) e -> p h s u e", h=2)
        for h in range(2):
            nc.vector.tensor_copy(k_places[h][:, :, :, :, 2], third_halves[:, h])
        turned_late = psum.tile([P, 2, 2, P], F32, name="turned_late", tag="bank_a2")
        turn(dealt_words(third[:]), turned_late[:, 0])
        last = place("last", [P, SLOTS], BF16, PAIR_AT)
        nc.vector.tensor_copy(last[:, :HALF], listed(planes[3], 0, HALF))
        nc.scalar.activation(last[:, HALF:], listed(planes[3], HALF, SLOTS), ACT.Copy)
        for h in range(2):
            nc.vector.tensor_copy(k_quads[h][:, :, 3], last[:, h * HALF : (h + 1) * HALF])
        turn(last[:].bitcast(F32).rearrange("p (s u) -> p u s", u=2), turned_late[:, 1])

        q_quads = [place("q_quads0", [P, P, PACK], BF16, Q_QUADS0_AT), place("q_quads1", [P, P, PACK], BF16, Q_QUADS1_AT)]

        def weave_queries(b, rows):
            nc.scalar.copy(
                q_quads[b][:].rearrange("p (c i) j -> p c j i", i=PACK)[:, :, rows],
                q_raw[:, rows, b * P : (b + 1) * P].rearrange("p j (c i) -> p c j i", i=PACK),
            )

        weave_queries(0, slice(0, 2))
        weave_queries(0, slice(2, 4))
        weave_queries(1, slice(0, 4))
        ts_column = place("ts_column", [P, PACK], F32, TS_COLUMN_AT)
        nc.scalar.copy(ts_column[:], ts_turned[:, :, 0])
        v_late, v_late_pairs = value_tile("v_late", V_LATE_AT)
        copy_values(v_late_pairs, turned_late[:])

        keys = [
            operand("k0", HALF, LAST_PLANE_AT + KIB),
            operand("k1", HALF, LAST_PLANE_AT + 2 * KIB, Q_QUADS0_AT),
        ]
        queries = [operand(f"q{b}", P, LAST_PLANE_AT + KIB * (b + 3)) for b in range(BLOCKS)]
        quantize(keys[0], k_quads[0][:])
        quantize(queries[0], q_quads[0][:])
        for lo in (0, P):
            quantize(keys[1], k_quads[1][:, lo : lo + P], slice(lo, lo + P))
        quantize(queries[1], q_quads[1][:])
        quarters = [(b, h) for b in range(BLOCKS) for h in range(2)]
        scores = {}
        pieces = [(0, 0, P, "bank_a0"), (0, P, HALF, "bank_b00"), (0, HALF, HALF + P, "bank_a3"), (0, HALF + P, SLOTS, "bank_b01")]
        pieces += [(1, 0, HALF, "bank_b10"), (1, HALF, HALF + P, "bank_b11"), (1, HALF + P, SLOTS, "bank_a1")]
        for b, first, end, bank in pieces:
            h, lo = divmod(first, HALF)
            scores[b, first] = psum.tile([P, end - first], F32, name=f"scores{b}_{first}", tag=bank)
            product(scores[b, first][:], queries[b], keys[h], slice(lo, lo + end - first))

        capped = [place("capped0", [P, PACK, P], F32), place("capped1", [P, PACK, P], F32, CAPPED1_AT)]
        scaled = {}
        for b, h in quarters:
            scaled[b, h] = place(f"scaled{b}{h}", [P, HALF], F32, FIRST_SCALED_AT if (b, h) == quarters[0] else None)
            cuts = (0, HALF) if (b, h) == (1, 0) else (0, HALF // 2, HALF)
            for lo, hi in zip(cuts, cuts[1:]):
                first, end = h * HALF + lo, h * HALF + hi
                start = first if (b, first) in scores else h * HALF
                source = scores[b, start][:, first - start : end - start]
                nc.vector.tensor_tensor(scaled[b, h][:, lo:hi], source, ts_rows[:, first:end], ALU.mult)
                nc.scalar.activation(
                    capped[b][:].rearrange("q t s -> q s t")[:, first // PACK : end // PACK],
                    scaled[b, h][:, lo:hi].rearrange("q (s t) -> q s t", t=PACK),
                    ACT.Tanh,
                    scale=1.0 / CAP,
                )
        minus_c, minus_m = [], []
        for b, at in enumerate((None, MINUS_C1_AT)):
            minus_c.append(place(f"minus_c{b}", [P, PACK, P], F32, at))
            minus_m.append(keep.tile([P, 1], F32, name=f"minus_m{b}"))
            nc.vector.tensor_scalar(
                minus_c[b][:], capped[b][:], -CAP, None, ALU.mult, ALU.min, accum_out=minus_m[b][:]
            )
        values = [operand(f"v{h}", HALF, scales_at=CAPPED1_AT + HALF * h) for h in range(2)]
        for h in range(2):
            for n, quads in enumerate((v_early, v_late)):
                quantize(values[h], quads[:, h], slice(n * P, (n + 1) * P))
        total = keep.tile([P, BLOCKS, len(EXP_PARTS)], F32, name="total")
        p_turned = []
        for b in range(BLOCKS):
            p_turned.append(psum.tile([P, PACK, P], F32, name=f"p_turned{b}", tag=f"bank_a{b}"))
            for n, (lo, hi) in enumerate(EXP_PARTS):
                prob = keep.tile([P, hi - lo, P], F32, name=f"prob{b}{n}")
                nc.scalar.activation(
                    prob[:],
                    minus_c[b][:, lo:hi],
                    ACT.Exp,
                    bias=minus_m[b][:],
                    scale=-1.0,
                    accum_out=total[:, b, n : n + 1],
                )
                for t in range(lo, hi):
                    nc.tensor.transpose(p_turned[b][:, t, :], prob[:, t - lo, :], ident[:])
        part_sum = place("part_sum", [P, BLOCKS], F32, MINUS_C1_AT)
        row_sum = keep.tile([P, BLOCKS], F32, name="row_sum")
        for b in range(BLOCKS):
            nc.scalar.activation(part_sum[:, b : b + 1], total[:, b, 0:1], ACT.Identity, bias=total[:, b, 1:2])
        for b in range(BLOCKS):
            nc.scalar.activation(row_sum[:, b : b + 1], part_sum[:, b : b + 1], ACT.Identity, bias=total[:, b, 2:3])
        w_quads = [place(f"w_quads{b}", [P, P, PACK], BF16) for b in range(BLOCKS)]
        weights = [operand(f"w{b}", P) for b in range(BLOCKS)]

        def weigh(b, lo, hi):
            nc.vector.tensor_tensor(
                w_quads[b][:, lo:hi],
                p_turned[b][:].rearrange("s t q -> s q t")[:, lo:hi],
                ts_column[:].unsqueeze(1).to_broadcast([P, hi - lo, PACK]),
                ALU.mult,
            )

        weigh(0, 0, P // 2)
        weigh(0, P // 2, P)
        quantize(weights[0], w_quads[0][:, : P // 2], slice(0, P // 2))
        weigh(1, 0, P // 2)
        quantize(weights[0], w_quads[0][:, P // 2 :], slice(P // 2, P))
        weigh(1, P // 2, P)
        quantize(weights[1], w_quads[1][:, : P // 2], slice(0, P // 2))
        inverse = keep.tile([P, BLOCKS], F32, name="inverse")
        nc.vector.reciprocal(inverse[:], row_sum[:])
        quantize(weights[1], w_quads[1][:, P // 2 :], slice(P // 2, P))
        y = {}
        for b, h in quarters:
            y[b, h] = psum.tile([P, PACK, P // 2], F32, name=f"y{b}{h}", tag=f"bank_b{b}{h}")
            product(y[b, h][:].rearrange("q j p -> q (j p)"), weights[b], values[h])

        results = [place("result0", [P, FEATURES], F32, TS_COLUMN_AT), place("result1", [P, FEATURES], F32)]
        for b, h in quarters:
            columns = slice(h * HALF, (h + 1) * HALF)
            nc.vector.scalar_tensor_tensor(
                results[b][:, columns].rearrange("q (p j) -> q p j", j=PACK),
                y[b, h][:].rearrange("q j p -> q p j"),
                inverse[:, b : b + 1],
                channel[:, columns].rearrange("q (p j) -> q p j", j=PACK),
                ALU.mult,
                ALU.mult,
            )
            nc.sync.dma_start(out[0, b * P : (b + 1) * P, columns], results[b][:, columns])
